import numpy as np
import ml_dtypes


def mxq(x, axis, fmt="e4m3"):
    dtype, down = {"e4m3": (ml_dtypes.float8_e4m3fn, 7), "e5m2": (ml_dtypes.float8_e5m2, 14)}[fmt]
    v = np.moveaxis(np.asarray(x, np.float32).astype(ml_dtypes.bfloat16).astype(np.float64), axis, -1)
    blocks = v.reshape(v.shape[:-1] + (-1, 32))
    amax = np.abs(blocks).max(-1, keepdims=True)
    byte = np.maximum(np.where(amax > 0, np.frexp(amax)[1] - 1 + 127, 0) - down, 1)
    scale = np.exp2(byte - 127.0)
    codes = (blocks / scale).astype(np.float32).astype(dtype).astype(np.float64)
    return np.moveaxis((codes * scale).reshape(v.shape), -1, axis)


WIDE = False


def mx_kscale(k):
    if not WIDE:
        return np.ones(k)
    levels = np.array([10, -10, 5, -5, 0])
    if k % 512:
        return np.exp2(np.random.permutation(np.resize(levels, k // 32))).repeat(32)
    a = np.empty((k // 512, 16))
    for p in range(k // 512):
        a[p, :8] = np.random.permutation(np.resize(levels, 8))
        for g in range(8):
            far = levels[np.abs(levels - a[p, g]) >= 10]
            a[p, g + 8] = far[np.random.randint(len(far))]
    return np.exp2(a.ravel()).repeat(32)


BF16 = ml_dtypes.bfloat16


def bf(x):
    return np.asarray(x, np.float32).astype(BF16)


def f64(x):
    return np.asarray(x).astype(np.float64)


E2M1 = np.array([0.0, 0.5, 1.0, 1.5, 2.0, 3.0, 4.0, 6.0, -0.0, -0.5, -1.0, -1.5, -2.0, -3.0, -4.0, -6.0])


def pack_weight(w, fmt):
    k, n = w.shape
    w = f64(bf(w)).reshape(k // 32, 32, n)
    amax = np.abs(w).max(1)
    if fmt == "e4m3":
        byte = np.frexp(amax)[1] - 1 + 127 - 7
    else:
        mant, ex = np.frexp(amax / 6.0)
        byte = np.where(mant > 0.5, ex, ex - 1) + 127
    byte = np.clip(np.where(amax > 0, byte, 1), 1, 254)
    scaled = (w * np.exp2(127.0 - byte)[:, None, :]).reshape(k, n).astype(np.float32)
    by_word = np.ascontiguousarray(scaled.reshape(k // 512, 128, 4, n).transpose(0, 1, 3, 2))
    if fmt == "e4m3":
        words = by_word.astype(ml_dtypes.float8_e4m3fn).view(np.uint8)
    else:
        c = by_word.astype(ml_dtypes.float4_e2m1fn).view(np.uint8) & 0xF
        words = c[..., 0::2] | (c[..., 1::2] << 4)
    return np.ascontiguousarray(words), np.ascontiguousarray(byte.astype(np.uint8).reshape(k // 512, 16, n))


def unpack_weight(words, scales, fmt):
    g, p, n, _ = words.shape
    if fmt == "e4m3":
        vals = np.ascontiguousarray(words).view(ml_dtypes.float8_e4m3fn).astype(np.float64)
    else:
        nib = np.empty((g, p, n, 4), np.uint8)
        nib[..., 0::2] = words & 0xF
        nib[..., 1::2] = words >> 4
        vals = E2M1[nib]
    vals = vals * np.repeat(np.exp2(scales.astype(np.float64) - 127.0), 8, axis=1)[..., None]
    return vals.transpose(0, 1, 3, 2).reshape(g * 512, n)
def pack4(w):
    words, scales = pack_weight(w, "e2m1")
    return words.reshape(words.shape[0], 128, -1), scales


def unpack4(words, scales):
    return unpack_weight(words.reshape(words.shape[0], 128, -1, 2), scales, "e2m1")


def planes(Y):
    n, m = Y.shape
    b = f64(bf(Y)).reshape(n // 32, 32, m)
    amax = np.abs(b).max(1)
    byte = np.clip(np.where(amax > 0, np.frexp(amax)[1] - 1 + 127 - 7, 1), 1, 254)
    codes = (b * np.exp2(127.0 - byte)[:, None, :]).reshape(n, m).astype(np.float32).astype(ml_dtypes.float8_e4m3fn).view(np.uint8)
    words = codes.reshape(n // 512, 128, 4, m).transpose(0, 1, 3, 2)
    return np.ascontiguousarray(words), np.ascontiguousarray(byte.astype(np.uint8).reshape(n // 512, 16, m))


G, T, C, F, N = 4, 1024, 512, 512, 512
LOGMAG_STD, PHASE_STD = 0.5, 0.8


def setup_inputs():
    s = mx_kscale(C)
    t = mx_kscale(F)
    x = np.random.randn(T, C) * s
    spread = np.repeat([LOGMAG_STD, PHASE_STD], F) / np.sqrt(C)
    w = np.random.randn(G, C, 2 * F) * spread / s[:, None]
    amp = np.exp(0.3 * np.random.randn(G, F)) * t
    basis = np.random.randn(G, F, N) / np.sqrt(F) / t[:, None]
    w_words, w_scales = pack4(w.reshape(G * C, 2 * F))
    b_words, b_scales = pack4(basis.reshape(G * F, N))
    r = 0.5 * np.random.randn(G, T, N)
    gain = np.exp(0.8 * np.random.randn(G, N))
    return {"x": bf(x), "w_words": w_words, "w_scales": w_scales, "amp": bf(amp),
            "b_words": b_words, "b_scales": b_scales, "r": bf(r), "gain": bf(gain)}


def reference(x, w_words, w_scales, amp, b_words, b_scales, r, gain):
    xq = mxq(f64(x), 1, "e4m3")
    w = unpack4(w_words, w_scales).reshape(G, C, 2 * F)
    basis = unpack4(b_words, b_scales).reshape(G, F, N)
    z = xq @ w
    h = f64(amp)[:, None, :] * np.exp(z[:, :, :F]) * np.cos(z[:, :, F:])
    o = mxq(h, 2, "e4m3") @ basis
    y = f64(gain)[:, None, :] * (o + f64(r))
    Y = y.transpose(2, 0, 1).reshape(N, G * T)
    words, scales = planes(Y)
    return y, words, scales

@@ -1,0 +1,349 @@
+import math
+from contextlib import ExitStack
+
+import concourse.mybir as mybir
+from concourse.masks import make_identity
+
+G, T, C, F, N = 4, 1024, 512, 512, 512
+FLOPS = 2 * G * T * C * 2 * F + 2 * G * T * F * N
+
+F32 = mybir.dt.float32
+BF16 = mybir.dt.bfloat16
+I32 = mybir.dt.int32
+U32 = mybir.dt.uint32
+U8 = mybir.dt.uint8
+FP8X4 = mybir.dt.float8_e4m3fn_x4
+FP4X4 = mybir.dt.float4_e2m1fn_x4
+ALU = mybir.AluOpType
+ACT = mybir.ActivationFunctionType
+
+P = 128
+PACK = 4
+FR = 512
+STEPS = G * T // FR
+LOGMAG, PHASE = 0, 1
+INV_2PI = 1.0 / (2.0 * math.pi)
+BANKS = {"phase": 3, "synth": 2, "side": 3}
+QUARTER = 0.25 + 2.0 ** -25
+
+
+def tile_banded_cosine_vocoder_head_k7_kernel(
+    tc, x, w_words, w_scales, amp, b_words, b_scales, r, gain, out_0, out_1, out_2
+):
+    nc = tc.nc
+    with ExitStack() as ctx:
+        keep = ctx.enter_context(tc.tile_pool(name="keep", bufs=1))
+        work = ctx.enter_context(tc.tile_pool(name="work", bufs=2))
+        psum = ctx.enter_context(tc.psum_pool(name="psum", bufs=1))
+        ctx.enter_context(tc.manual_schedule())
+
+        def kept(name, shape, dtype):
+            return keep.tile(shape, dtype, name=name, tag=name, align_bytes=64)
+
+        def rotating(tag, shape, dtype, bufs):
+            return work.tile(shape, dtype, name=tag, tag=tag, bufs=bufs, align_bytes=64)
+
+        def bank(tag):
+            return psum.tile([P, 512], F32, name=tag, tag=tag, bufs=BANKS[tag])
+
+        amp_raw = kept("amp_raw", [P, G, PACK], BF16)
+        ws_raw = kept("ws_raw", [P, G, 2 * F], U8)
+        wc_raw = [kept("wc_raw%d" % u, [P, 4 * F], U8) for u in range(G)]
+        x_raw = [[kept("x_raw%d%d" % (hf, g), [P, 2, C], BF16) for g in range(2)] for hf in range(2)]
+        b_codes = kept("b_codes", [P, G, 2 * N], U8)
+        b_scale = kept("b_scale", [P, G, N], U8)
+        gain_all = kept("gain_all", [P, G * N], BF16)
+        r_sb = [kept("r_sb%d" % s, [P, 2, 2, N], BF16) for s in range(STEPS)]
+        ident = kept("ident", [P, P], F32)
+
+        nc.vector.memset(ws_raw[:].rearrange("p u n -> p (u n)").bitcast(I32), 0)
+        make_identity(nc, ident[:])
+        nc.gpsimd.memset(b_scale[:].rearrange("p u n -> p (u n)").bitcast(I32), 0)
+
+        def frames_of(dram, hf):
+            return dram[hf * FR:(hf + 1) * FR, :].rearrange("(g p j) c -> p g j c", g=2, j=2)
+
+        def load_scale_rows(plane, rows):
+            for q in range(4):
+                nc.sync.dma_start(out=plane[32 * q:32 * q + 4, :, :].bitcast(I32),
+                                  in_=rows[:, 4 * q:4 * q + 4, :].rearrange("u r n -> r u n").bitcast(I32))
+
+        nc.sync.dma_start(out=amp_raw[:], in_=amp.rearrange("u (p t) -> p u t", t=PACK))
+        for g in range(2):
+            nc.sync.dma_start(out=x_raw[0][g][:], in_=frames_of(x, 0)[:, g, :, :])
+        nc.sync.dma_start(out=wc_raw[0][:].bitcast(I32), in_=w_words[0].bitcast(I32))
+        load_scale_rows(ws_raw, w_scales)
+        for g in range(2):
+            nc.sync.dma_start(out=x_raw[1][g][:], in_=frames_of(x, 1)[:, g, :, :])
+        for u in range(1, G):
+            nc.sync.dma_start(out=wc_raw[u][:].bitcast(I32), in_=w_words[u].bitcast(I32))
+        load_scale_rows(b_scale, b_scales)
+        nc.sync.dma_start(out=b_codes[:].bitcast(I32), in_=b_words.rearrange("u p n -> p u n").bitcast(I32))
+        nc.sync.dma_start(out=gain_all[:], in_=gain.rearrange("u n -> (u n)").partition_broadcast(P))
+        for s in range(STEPS):
+            nc.sync.dma_start(out=r_sb[s][:], in_=frames_of(r[s // 2], s % 2))
+
+        amp32 = kept("amp32", [P, G * PACK], F32)
+        mant = kept("mant", [P, G * PACK], I32)
+        expo = kept("expo", [P, G * PACK], I32)
+        expo_ln = kept("expo_ln", [P, G * PACK], F32)
+        mant_ln = kept("mant_ln", [P, G * PACK], F32)
+        log_amp = kept("log_amp", [P, G * PACK], F32)
+        sgn = kept("sgn", [P, G * PACK], F32)
+        sin_scale = kept("sin_scale", [P, G * PACK], F32)
+        sin_bias = kept("sin_bias", [P, G * PACK], F32)
+        nc.vector.tensor_copy(out=amp32[:], in_=amp_raw[:].rearrange("p u t -> p (u t)"))
+        nc.vector.tensor_scalar(out=mant[:], in0=amp32[:].bitcast(I32), scalar1=0x007FFFFF, scalar2=0x3F800000,
+                                op0=ALU.bitwise_and, op1=ALU.bitwise_or)
+        nc.vector.tensor_scalar(out=expo[:], in0=amp32[:].bitcast(I32), scalar1=23, scalar2=0xFF,
+                                op0=ALU.logical_shift_right, op1=ALU.bitwise_and)
+        nc.vector.tensor_scalar(out=expo_ln[:], in0=expo[:], scalar1=-127.0, scalar2=math.log(2.0),
+                                op0=ALU.add, op1=ALU.mult)
+        nc.scalar.activation(out=mant_ln[:], in_=mant[:].bitcast(F32), func=ACT.Ln)
+        nc.scalar.activation(out=sgn[:], in_=amp32[:], func=ACT.Sign)
+        nc.scalar.activation(out=sin_scale[:], in_=sgn[:], func=ACT.Copy, scale=2.0 * math.pi)
+        nc.scalar.activation(out=sin_bias[:], in_=sgn[:], func=ACT.Copy, scale=0.5 * math.pi)
+        nc.gpsimd.tensor_tensor(out=log_amp[:], in0=mant_ln[:], in1=expo_ln[:], op=ALU.add)
+
+        w_codes = [kept("w_codes%d" % u, [P, 2, 2 * F], U8) for u in range(G)]
+        w_scale = [kept("w_scale%d" % u, [P, 2, F], U8) for u in range(G)]
+
+        def sort_w_scale(u):
+            nc.vector.tensor_copy(out=w_scale[u][:].rearrange("p h (t c i) -> p h c t i", t=PACK, i=16),
+                                  in_=ws_raw[:, u, :].rearrange("p (h c i t) -> p h c t i", h=2, t=PACK, i=16))
+
+        def sort_w_codes(u, half):
+            nc.vector.tensor_copy(
+                out=w_codes[u][:, half, :].rearrange("p (t c i b) -> p c t i b", t=PACK, i=8, b=2),
+                in_=wc_raw[u][:, half * 2 * F:(half + 1) * 2 * F].rearrange("p (c i t b) -> p c t i b", t=PACK, i=8, b=2))
+
+        x_grp = [kept("x_grp%d" % hf, [P, FR * PACK], BF16) for hf in range(2)]
+        x_codes = [kept("x_codes%d" % hf, [P, FR], U32) for hf in range(2)]
+        x_scale = [kept("x_scale%d" % hf, [P, FR], U8) for hf in range(2)]
+
+        def turn_x(hf, g):
+            tb = bank("side")
+            tv = tb[:].rearrange("p (j u r) -> p j u r", j=2, u=2)
+            for j in range(2):
+                words = x_raw[hf][g][:, j, :].bitcast(F32)
+                for u in range(2):
+                    nc.tensor.transpose(tv[:, j, u, :], words[:, u:256:2], ident[:])
+            return tv
+
+        def group_x(hf, g, tv, copy):
+            dst = x_grp[hf][:, 1024 * g:1024 * (g + 1)].bitcast(F32).rearrange("p (j r u) -> p j r u", j=2, u=2)
+            copy(out=dst, in_=tv.rearrange("p j u r -> p j r u"))
+
+        def quantize_x(hf):
+            nc.vector.quantize_mx(out=x_codes[hf][:].bitcast(FP8X4), scales=x_scale[hf][:], in_=x_grp[hf][:])
+
+        def project(s, half, t, tag):
+            u, hf = divmod(s, 2)
+            zb = bank(tag)
+            nc.tensor.matmul_mx(out=zb[:], lhsT=w_codes[u][:, half, 256 * t:256 * (t + 1)].bitcast(FP4X4),
+                                lhsT_scale=w_scale[u][:, half, P * t:P * (t + 1)],
+                                rhs=x_codes[hf][:].bitcast(FP8X4), rhs_scale=x_scale[hf][:], start=True, stop=True)
+            return zb
+
+        mag, wave, hq, hs, y_sb, y_bf, y_grp = {}, {}, {}, {}, {}, {}, {}
+        y_scale = kept("y_scale", [P, G * T], U8)
+
+        def magnitude(s, t):
+            if t == 0:
+                mag[s] = rotating("mag", [P, PACK, FR], F32, 5)
+            zb = project(s, LOGMAG, t, "side")
+            col = PACK * (s // 2) + t
+            nc.scalar.activation(out=mag[s][:, t, :], in_=zb[:], func=ACT.Exp, bias=log_amp[:, col:col + 1])
+
+        def turns(s, t):
+            zb = project(s, PHASE, t, "phase")
+            whole = rotating("whole", [P, FR], I32, 3)
+            nc.vector.tensor_scalar(out=whole[:], in0=zb[:], scalar1=INV_2PI, scalar2=QUARTER, op0=ALU.mult, op1=ALU.add)
+            return zb, whole
+
+        def reduce_phase(s, t, zb, whole):
+            if t == 0:
+                wave[s] = rotating("wave", [P, PACK, FR], F32, 2)
+            nc.vector.scalar_tensor_tensor(out=wave[s][:, t, :], in0=zb[:], scalar=INV_2PI, in1=whole[:],
+                                           op0=ALU.mult, op1=ALU.subtract)
+
+        def cosines(s):
+            u = s // 2
+            for t in range(PACK):
+                col = PACK * u + t
+                nc.scalar.activation(out=wave[s][:, t, :], in_=wave[s][:, t, :], func=ACT.Sin,
+                                     scale=sin_scale[:, col:col + 1], bias=sin_bias[:, col:col + 1])
+
+        h_grp = {}
+
+        def make_h(s, lo, hi, engine):
+            if lo == 0:
+                h_grp[s] = rotating("h_grp", [P, FR, PACK], BF16, 1)
+            engine.tensor_tensor(out=h_grp[s][:, lo:hi, :].rearrange("p (c i) t -> p c t i", i=4),
+                                    in0=mag[s][:, :, lo:hi].rearrange("p t (c i) -> p c t i", i=4),
+                                    in1=wave[s][:, :, lo:hi].rearrange("p t (c i) -> p c t i", i=4), op=ALU.mult)
+
+        def quantize_h(s, lo, hi):
+            if lo == 0:
+                hq[s] = rotating("h_codes", [P, FR], U32, 2)
+                hs[s] = rotating("h_scale", [P, FR], U8, 2)
+            nc.vector.quantize_mx(out=hq[s][:, lo:hi].bitcast(FP8X4), scales=hs[s][:, lo:hi],
+                                  in_=h_grp[s][:, lo:hi, :].rearrange("p c t -> p (c t)"))
+
+        def synthesize(s, jj):
+            u = s // 2
+            g, j = divmod(jj, 2)
+            ob = bank("synth")
+            nc.tensor.matmul_mx(out=ob[:], lhsT=hq[s][:, P * jj:P * (jj + 1)].bitcast(FP8X4),
+                                lhsT_scale=hs[s][:, P * jj:P * (jj + 1)],
+                                rhs=b_codes[:, u, :].bitcast(FP4X4), rhs_scale=b_scale[:, u, :], start=True, stop=True)
+            summed = rotating("summed", [P, N], F32, 8)
+            nc.vector.tensor_tensor(out=summed[:], in0=ob[:], in1=r_sb[s][:, g, j, :], op=ALU.add)
+            return summed
+
+        def apply_gain(s, jj, summed, engine):
+            u, hf = divmod(s, 2)
+            g, j = divmod(jj, 2)
+            if jj == 0:
+                y_sb[s] = rotating("y_sb", [P, 2, 2, N], F32, 3)
+            engine.tensor_tensor(out=y_sb[s][:, g, j, :], in0=summed[:], in1=gain_all[:, u * N:(u + 1) * N], op=ALU.mult)
+            if j == 1:
+                nc.sync.dma_start(out=frames_of(out_0[u], hf)[:, g, :, :], in_=y_sb[s][:, g, :, :])
+
+        def round_y(s, jj, copy):
+            g, j = divmod(jj, 2)
+            if jj == 0:
+                y_bf[s] = rotating("y_bf", [P, 4, N], BF16, 2)
+            copy(out=y_bf[s][:, jj, :].rearrange("p (u m e) -> p u m e", u=2, e=2),
+                 in_=y_sb[s][:, g, j, :].rearrange("p (m u e) -> p u m e", u=2, e=2))
+
+        turned = {}
+
+        def turn_y(s, g):
+            tb = bank("side")
+            turned[s, g] = tb[:].rearrange("p (j u r) -> p j u r", j=2, u=2)
+            for j in range(2):
+                words = y_bf[s][:, 2 * g + j, :].bitcast(F32)
+                for u in range(2):
+                    nc.tensor.transpose(turned[s, g][:, j, u, :], words[:, P * u:P * (u + 1)], ident[:])
+
+        def group_y(s, g):
+            if g == 0:
+                y_grp[s] = rotating("y_grp", [P, FR * PACK], BF16, 3)
+            dst = y_grp[s][:, 1024 * g:1024 * (g + 1)].bitcast(F32).rearrange("p (r j u) -> p r j u", j=2, u=2)
+            nc.scalar.copy(out=dst, in_=turned[s, g].rearrange("p j u r -> p r j u"))
+
+        def planes_in(s):
+            copy = nc.scalar.copy
+            return [(round_y, s, 0, copy), (round_y, s, 1, copy), (round_y, s, 2, copy), (turn_y, s, 0),
+                    (round_y, s, 3, copy), (group_y, s, 0), (turn_y, s, 1), (group_y, s, 1)]
+
+        def magnitudes(s):
+            return [(magnitude, s, t) for t in range(PACK)]
+
+        def write(tasks, count):
+            for unused in range(min(count, len(tasks))):
+                call, *args = tasks.pop(0)
+                call(*args)
+
+        words_out = out_1[0].rearrange("p m t -> p (m t)")
+
+        def quantize_y(s, lo, hi):
+            y_codes = rotating("y_codes", [P, FR], U32, 3)
+            nc.vector.quantize_mx(out=y_codes[:, lo:hi].bitcast(FP8X4), scales=y_scale[:, FR * s + lo:FR * s + hi],
+                                  in_=y_grp[s][:, PACK * lo:PACK * hi])
+            nc.sync.dma_start(out=words_out[:, PACK * (FR * s + lo):PACK * (FR * s + hi)].bitcast(I32),
+                              in_=y_codes[:, lo:hi].bitcast(I32))
+
+        def store_scales(lo, hi):
+            for q in range(4):
+                nc.sync.dma_start(out=out_2[0, 4 * q:4 * q + 4, lo:hi].bitcast(I32),
+                                  in_=y_scale[32 * q:32 * q + 4, lo:hi].bitcast(I32))
+
+        def psum_work(s, beside):
+            back = s - 2
+            held = {}
+
+            def synth(jj):
+                apply_gain(back, jj, synthesize(back, jj), nc.gpsimd)
+
+            def turn(t):
+                held[t] = turns(s, t)
+
+            def rest(t):
+                reduce_phase(s, t, *held[t])
+
+            order = [(turn, 0), (turn, 1), (synth, 0), (rest, 0), (synth, 1), (turn, 2), (synth, 2), (rest, 1),
+                     (synth, 3), (turn, 3), (rest, 2), (rest, 3)]
+            for call, index in order:
+                if call != synth or back >= 0:
+                    call(index)
+                    write(beside, 1)
+            write(beside, len(beside))
+
+        def sbuf_work(s):
+            make_h(s - 1, 0, FR, nc.vector)
+            if s >= 4:
+                quantize_y(s - 4, 0, FR)
+            quantize_h(s - 1, 0, FR)
+
+        x00 = turn_x(0, 0)
+        group_x(0, 0, x00, nc.vector.tensor_copy)
+        x01 = turn_x(0, 1)
+        group_x(0, 1, x01, nc.vector.tensor_copy)
+        sort_w_codes(0, LOGMAG)
+        quantize_x(0)
+        sort_w_scale(0)
+        sort_w_codes(0, PHASE)
+        x10 = turn_x(1, 0)
+        magnitude(0, 0)
+        group_x(1, 0, x10, nc.scalar.copy)
+        x11 = turn_x(1, 1)
+        group_x(1, 1, x11, nc.scalar.copy)
+        sort_w_scale(1)
+        sort_w_codes(1, LOGMAG)
+        magnitude(0, 1)
+        quantize_x(1)
+        psum_work(0, magnitudes(0)[2:] + magnitudes(1) + magnitudes(2)[:2])
+        psum_work(1, magnitudes(2)[2:] + magnitudes(3))
+        cosines(0)
+        cosines(1)
+        sort_w_codes(1, PHASE)
+        for u in range(2, G):
+            sort_w_scale(u)
+            sort_w_codes(u, LOGMAG)
+            sort_w_codes(u, PHASE)
+        sbuf_work(1)
+
+        beside = {2: magnitudes(4) + magnitudes(5), 3: planes_in(0), 4: magnitudes(6) + magnitudes(7),
+                  5: planes_in(1) + planes_in(2), 6: planes_in(3), 7: planes_in(4)}
+        for s in range(2, STEPS):
+            psum_work(s, beside[s])
+            cosines(s)
+            sbuf_work(s)
+
+        last = STEPS - 1
+        write(planes_in(last - 2), 8)
+        make_h(last, 0, FR // 2, nc.vector)
+        make_h(last, FR // 2, FR, nc.vector)
+        quantize_h(last, 0, FR // 2)
+        quantize_y(last - 3, 0, FR)
+        quantize_h(last, FR // 2, FR)
+        for jj in range(4):
+            apply_gain(last - 1, jj, synthesize(last - 1, jj), nc.gpsimd)
+        sums = [synthesize(last, jj) for jj in range(4)]
+        write(planes_in(last - 1), 6)
+        quantize_y(last - 2, 0, FR)
+        store_scales(0, FR * (last - 1))
+        write(planes_in(last - 1)[6:], 2)
+        for g in range(2):
+            for jj in (2 * g, 2 * g + 1):
+                apply_gain(last, jj, sums[jj], nc.vector)
+            for jj in (2 * g, 2 * g + 1):
+                round_y(last, jj, nc.vector.tensor_copy)
+            turn_y(last, g)
+            group_y(last, g)
+        quantize_y(last - 1, 0, FR)
+        quantize_y(last, 0, FR // 2)
+        quantize_y(last, FR // 2, FR)
+        store_scales(FR * (last - 1), FR * STEPS)

@@ -24,6 +24,7 @@ STEPS = G * T // FR
 LOGMAG, PHASE = 0, 1
 INV_2PI = 1.0 / (2.0 * math.pi)
 BANKS = {"phase": 3, "synth": 2, "side": 3}
+SHARES = {2: 256, 3: 0, 4: 128, 5: 0, 6: 128, 7: 128}
 QUARTER = 0.25 + 2.0 ** -25
 
 
@@ -155,50 +156,74 @@ def tile_banded_cosine_vocoder_head_k7_kernel(
             col = PACK * (s // 2) + t
             nc.scalar.activation(out=mag[s][:, t, :], in_=zb[:], func=ACT.Exp, bias=log_amp[:, col:col + 1])
 
-        def turns(s, t):
-            zb = project(s, PHASE, t, "phase")
-            whole = rotating("whole", [P, FR], I32, 3)
-            nc.vector.tensor_scalar(out=whole[:], in0=zb[:], scalar1=INV_2PI, scalar2=QUARTER, op0=ALU.mult, op1=ALU.add)
-            return zb, whole
+        phase_todo = [(s, t) for s in range(STEPS) for t in range(PACK)]
+        phase_bank, whole = {}, {}
 
-        def reduce_phase(s, t, zb, whole):
+        def project_next_phase():
+            if phase_todo:
+                s, t = phase_todo.pop(0)
+                phase_bank[s, t] = project(s, PHASE, t, "phase")
+
+        def count_turns(s, t):
+            whole[s, t] = rotating("whole", [P, FR], I32, 3)
+            nc.vector.tensor_scalar(out=whole[s, t][:], in0=phase_bank[s, t][:], scalar1=INV_2PI, scalar2=QUARTER,
+                                    op0=ALU.mult, op1=ALU.add)
+
+        def reduce_phase(s, t):
             if t == 0:
                 wave[s] = rotating("wave", [P, PACK, FR], F32, 2)
-            nc.vector.scalar_tensor_tensor(out=wave[s][:, t, :], in0=zb[:], scalar=INV_2PI, in1=whole[:],
+            nc.vector.scalar_tensor_tensor(out=wave[s][:, t, :], in0=phase_bank[s, t][:], scalar=INV_2PI, in1=whole[s, t][:],
                                            op0=ALU.mult, op1=ALU.subtract)
+            project_next_phase()
 
-        def cosines(s):
-            u = s // 2
-            for t in range(PACK):
-                col = PACK * u + t
-                nc.scalar.activation(out=wave[s][:, t, :], in_=wave[s][:, t, :], func=ACT.Sin,
-                                     scale=sin_scale[:, col:col + 1], bias=sin_bias[:, col:col + 1])
+        def cosine(s, t):
+            col = PACK * (s // 2) + t
+            nc.scalar.activation(out=wave[s][:, t, :], in_=wave[s][:, t, :], func=ACT.Sin,
+                                 scale=sin_scale[:, col:col + 1], bias=sin_bias[:, col:col + 1])
 
         h_grp = {}
 
-        def make_h(s, lo, hi, engine):
-            if lo == 0:
+        def make_h(s, lo, hi):
+            if s not in h_grp:
                 h_grp[s] = rotating("h_grp", [P, FR, PACK], BF16, 1)
-            engine.tensor_tensor(out=h_grp[s][:, lo:hi, :].rearrange("p (c i) t -> p c t i", i=4),
+            nc.vector.tensor_tensor(out=h_grp[s][:, lo:hi, :].rearrange("p (c i) t -> p c t i", i=4),
                                     in0=mag[s][:, :, lo:hi].rearrange("p t (c i) -> p c t i", i=4),
                                     in1=wave[s][:, :, lo:hi].rearrange("p t (c i) -> p c t i", i=4), op=ALU.mult)
 
+        def make_h_share(s, hi):
+            h_grp[s] = rotating("h_grp", [P, FR, PACK], BF16, 1)
+            nc.gpsimd.tensor_tensor(out=h_grp[s][:, :hi, :], in0=mag[s][:, :, :hi].rearrange("p t c -> p c t"),
+                                    in1=wave[s][:, :, :hi].rearrange("p t c -> p c t"), op=ALU.mult)
+
         def quantize_h(s, lo, hi):
             if lo == 0:
-                hq[s] = rotating("h_codes", [P, FR], U32, 2)
-                hs[s] = rotating("h_scale", [P, FR], U8, 2)
+                hq[s] = rotating("h_codes", [P, FR], U32, 3)
+                hs[s] = rotating("h_scale", [P, FR], U8, 3)
             nc.vector.quantize_mx(out=hq[s][:, lo:hi].bitcast(FP8X4), scales=hs[s][:, lo:hi],
                                   in_=h_grp[s][:, lo:hi, :].rearrange("p c t -> p (c t)"))
+            synth_ready.extend((s, jj) for jj in range(lo // P, hi // P))
+            synthesize_next()
 
-        def synthesize(s, jj):
-            u = s // 2
+        synth_ready, synth_bank = [], {}
+        synth_free = ["synth"] * BANKS["synth"]
+
+        def synthesize_next():
+            while synth_ready and synth_free:
+                s, jj = synth_ready.pop(0)
+                tag = synth_free.pop(0)
+                synth_bank[s, jj] = tag, bank(tag)
+                nc.tensor.matmul_mx(out=synth_bank[s, jj][1][:], lhsT=hq[s][:, P * jj:P * (jj + 1)].bitcast(FP8X4),
+                                    lhsT_scale=hs[s][:, P * jj:P * (jj + 1)],
+                                    rhs=b_codes[:, s // 2, :].bitcast(FP4X4), rhs_scale=b_scale[:, s // 2, :],
+                                    start=True, stop=True)
+
+        def add_residual(s, jj):
             g, j = divmod(jj, 2)
-            ob = bank("synth")
-            nc.tensor.matmul_mx(out=ob[:], lhsT=hq[s][:, P * jj:P * (jj + 1)].bitcast(FP8X4),
-                                lhsT_scale=hs[s][:, P * jj:P * (jj + 1)],
-                                rhs=b_codes[:, u, :].bitcast(FP4X4), rhs_scale=b_scale[:, u, :], start=True, stop=True)
             summed = rotating("summed", [P, N], F32, 8)
+            tag, ob = synth_bank.pop((s, jj))
             nc.vector.tensor_tensor(out=summed[:], in0=ob[:], in1=r_sb[s][:, g, j, :], op=ALU.add)
+            synth_free.append(tag)
+            synthesize_next()
             return summed
 
         def apply_gain(s, jj, summed, engine):
@@ -233,11 +258,6 @@ def tile_banded_cosine_vocoder_head_k7_kernel(
             dst = y_grp[s][:, 1024 * g:1024 * (g + 1)].bitcast(F32).rearrange("p (r j u) -> p r j u", j=2, u=2)
             nc.scalar.copy(out=dst, in_=turned[s, g].rearrange("p j u r -> p r j u"))
 
-        def planes_in(s):
-            copy = nc.scalar.copy
-            return [(round_y, s, 0, copy), (round_y, s, 1, copy), (round_y, s, 2, copy), (turn_y, s, 0),
-                    (round_y, s, 3, copy), (group_y, s, 0), (turn_y, s, 1), (group_y, s, 1)]
-
         def magnitudes(s):
             return [(magnitude, s, t) for t in range(PACK)]
 
@@ -249,7 +269,7 @@ def tile_banded_cosine_vocoder_head_k7_kernel(
         words_out = out_1[0].rearrange("p m t -> p (m t)")
 
         def quantize_y(s, lo, hi):
-            y_codes = rotating("y_codes", [P, FR], U32, 3)
+            y_codes = rotating("y_codes", [P, FR], U32, 4)
             nc.vector.quantize_mx(out=y_codes[:, lo:hi].bitcast(FP8X4), scales=y_scale[:, FR * s + lo:FR * s + hi],
                                   in_=y_grp[s][:, PACK * lo:PACK * hi])
             nc.sync.dma_start(out=words_out[:, PACK * (FR * s + lo):PACK * (FR * s + hi)].bitcast(I32),
@@ -260,89 +280,115 @@ def tile_banded_cosine_vocoder_head_k7_kernel(
                 nc.sync.dma_start(out=out_2[0, 4 * q:4 * q + 4, lo:hi].bitcast(I32),
                                   in_=y_scale[32 * q:32 * q + 4, lo:hi].bitcast(I32))
 
-        def psum_work(s, beside):
-            back = s - 2
-            held = {}
+        def finish(s, jj):
+            apply_gain(s, jj, add_residual(s, jj), nc.gpsimd)
 
-            def synth(jj):
-                apply_gain(back, jj, synthesize(back, jj), nc.gpsimd)
+        def phases(s):
+            return [(count_turns, s, 0), (count_turns, s, 1), (reduce_phase, s, 0), (count_turns, s, 2),
+                    (reduce_phase, s, 1), (count_turns, s, 3), (reduce_phase, s, 2), (reduce_phase, s, 3)]
 
-            def turn(t):
-                held[t] = turns(s, t)
+        def finishes(groups):
+            return [(finish, s, 2 * g + j) for s, g in groups for j in range(2)]
 
-            def rest(t):
-                reduce_phase(s, t, *held[t])
+        def cosines(s):
+            return [(cosine, s, t) for t in range(PACK)]
 
-            order = [(turn, 0), (turn, 1), (synth, 0), (rest, 0), (synth, 1), (turn, 2), (synth, 2), (rest, 1),
-                     (synth, 3), (turn, 3), (rest, 2), (rest, 3)]
-            for call, index in order:
-                if call != synth or back >= 0:
-                    call(index)
-                    write(beside, 1)
-            write(beside, len(beside))
+        def roundings(groups):
+            return [(round_y, s, 2 * g + j, nc.scalar.copy) for s, g in groups for j in range(2)]
 
-        def sbuf_work(s):
-            make_h(s - 1, 0, FR, nc.vector)
+        def turnings(groups):
+            return [(turn_y, s, g) for s, g in groups] + [(group_y, s, g) for s, g in groups]
+
+        def groups_of(s):
+            return [divmod(n, 2) for n in (2 * s - 5, 2 * s - 4) if n >= 0]
+
+        def weave(first, second):
+            woven = []
+            for n in range(max(len(first), len(second))):
+                woven.extend(first[n:n + 1] + second[n:n + 1])
+            return woven
+
+        def write_all(tasks):
+            write(tasks, len(tasks))
+
+        x00 = turn_x(0, 0)
+        x01 = turn_x(0, 1)
+        group_x(0, 0, x00, nc.vector.tensor_copy)
+        sort_w_codes(0, LOGMAG)
+        group_x(0, 1, x01, nc.vector.tensor_copy)
+        x10 = turn_x(1, 0)
+        x11 = turn_x(1, 1)
+        sort_w_scale(0)
+        quantize_x(0)
+        sort_w_codes(0, PHASE)
+        magnitude(0, 0)
+        project_next_phase()
+        group_x(1, 0, x10, nc.scalar.copy)
+        group_x(1, 1, x11, nc.scalar.copy)
+        project_next_phase()
+        magnitude(0, 1)
+        project_next_phase()
+        sort_w_scale(1)
+        sort_w_codes(1, LOGMAG)
+        write_all(weave(phases(0)[:2], magnitudes(0)[2:]))
+        quantize_x(1)
+        write_all(weave(magnitudes(1) + magnitudes(2) + magnitudes(3), phases(0)[2:] + [(sort_w_codes, 1, PHASE)] + phases(1)))
+        write_all(cosines(0) + cosines(1))
+        for u in range(2, G):
+            sort_w_scale(u)
+            sort_w_codes(u, LOGMAG)
+        sort_w_codes(2, PHASE)
+
+        last = STEPS - 1
+
+        def sbuf_work(s, lo):
+            make_h(s - 1, lo, FR)
+            if s == 1:
+                sort_w_codes(3, PHASE)
             if s >= 4:
                 quantize_y(s - 4, 0, FR)
             quantize_h(s - 1, 0, FR)
 
-        x00 = turn_x(0, 0)
-        group_x(0, 0, x00, nc.vector.tensor_copy)
-        x01 = turn_x(0, 1)
-        group_x(0, 1, x01, nc.vector.tensor_copy)
-        sort_w_codes(0, LOGMAG)
-        quantize_x(0)
-        sort_w_scale(0)
-        sort_w_codes(0, PHASE)
-        x10 = turn_x(1, 0)
-        magnitude(0, 0)
-        group_x(1, 0, x10, nc.scalar.copy)
-        x11 = turn_x(1, 1)
-        group_x(1, 1, x11, nc.scalar.copy)
-        sort_w_scale(1)
-        sort_w_codes(1, LOGMAG)
-        magnitude(0, 1)
-        quantize_x(1)
-        psum_work(0, magnitudes(0)[2:] + magnitudes(1) + magnitudes(2)[:2])
-        psum_work(1, magnitudes(2)[2:] + magnitudes(3))
-        cosines(0)
-        cosines(1)
-        sort_w_codes(1, PHASE)
-        for u in range(2, G):
-            sort_w_scale(u)
-            sort_w_codes(u, LOGMAG)
-            sort_w_codes(u, PHASE)
-        sbuf_work(1)
-
-        beside = {2: magnitudes(4) + magnitudes(5), 3: planes_in(0), 4: magnitudes(6) + magnitudes(7),
-                  5: planes_in(1) + planes_in(2), 6: planes_in(3), 7: planes_in(4)}
+        sbuf_work(1, 0)
         for s in range(2, STEPS):
-            psum_work(s, beside[s])
-            cosines(s)
-            sbuf_work(s)
+            share = SHARES[s]
+            if share:
+                make_h_share(s - 1, share)
+            if s == 2:
+                own = phases(s)[:3] + weave(finishes(groups_of(s)), phases(s)[3:])
+            else:
+                own = weave(finishes(groups_of(s)), phases(s))
+            if s in (2, 4):
+                write_all(weave(own, magnitudes(s + 2) + magnitudes(s + 3)))
+                write_all(roundings(groups_of(s)) + cosines(s))
+            else:
+                write_all(own)
+                write_all(weave(roundings(groups_of(s)), cosines(s)))
+            write_all(turnings(groups_of(s)))
+            sbuf_work(s, share)
 
-        last = STEPS - 1
-        write(planes_in(last - 2), 8)
-        make_h(last, 0, FR // 2, nc.vector)
-        make_h(last, FR // 2, FR, nc.vector)
-        quantize_h(last, 0, FR // 2)
+        synth_free.extend(["phase"] * BANKS["phase"])
+        synthesize_next()
         quantize_y(last - 3, 0, FR)
+        make_h(last, 0, FR // 2)
+        make_h(last, FR // 2, FR)
+        quantize_h(last, 0, FR // 2)
         quantize_h(last, FR // 2, FR)
-        for jj in range(4):
-            apply_gain(last - 1, jj, synthesize(last - 1, jj), nc.gpsimd)
-        sums = [synthesize(last, jj) for jj in range(4)]
-        write(planes_in(last - 1), 6)
-        quantize_y(last - 2, 0, FR)
-        store_scales(0, FR * (last - 1))
-        write(planes_in(last - 1)[6:], 2)
-        for g in range(2):
+        on_gpsimd = [(last - 2, 1), (last - 1, 0)]
+        on_vector = [(last - 1, 1), (last, 0), (last, 1)]
+        write_all(finishes(on_gpsimd))
+        sums = {(s, jj): add_residual(s, jj) for s, g in on_vector for jj in (2 * g, 2 * g + 1)}
+        write_all(roundings(on_gpsimd) + turnings(on_gpsimd))
+        for s, g in on_vector:
             for jj in (2 * g, 2 * g + 1):
-                apply_gain(last, jj, sums[jj], nc.vector)
+                apply_gain(s, jj, sums[s, jj], nc.vector)
             for jj in (2 * g, 2 * g + 1):
-                round_y(last, jj, nc.vector.tensor_copy)
-            turn_y(last, g)
-            group_y(last, g)
+                round_y(s, jj, nc.scalar.copy if s < last else nc.vector.tensor_copy)
+            if s < last:
+                quantize_y(last - 2, 0, FR)
+                store_scales(0, FR * (last - 1))
+            turn_y(s, g)
+            group_y(s, g)
         quantize_y(last - 1, 0, FR)
         quantize_y(last, 0, FR // 2)
         quantize_y(last, FR // 2, FR)

@@ -24,7 +24,7 @@ STEPS = G * T // FR
 LOGMAG, PHASE = 0, 1
 INV_2PI = 1.0 / (2.0 * math.pi)
 BANKS = {"phase": 3, "synth": 2, "side": 3}
-SHARES = {2: 256, 3: 0, 4: 128, 5: 0, 6: 128, 7: 128}
+AHEAD = {2: (3, 4, 5), 4: (6, 7)}
 QUARTER = 0.25 + 2.0 ** -25
 
 
@@ -184,16 +184,11 @@ def tile_banded_cosine_vocoder_head_k7_kernel(
         h_grp = {}
 
         def make_h(s, lo, hi):
-            if s not in h_grp:
+            if lo == 0:
                 h_grp[s] = rotating("h_grp", [P, FR, PACK], BF16, 1)
             nc.vector.tensor_tensor(out=h_grp[s][:, lo:hi, :].rearrange("p (c i) t -> p c t i", i=4),
                                     in0=mag[s][:, :, lo:hi].rearrange("p t (c i) -> p c t i", i=4),
                                     in1=wave[s][:, :, lo:hi].rearrange("p t (c i) -> p c t i", i=4), op=ALU.mult)
-
-        def make_h_share(s, hi):
-            h_grp[s] = rotating("h_grp", [P, FR, PACK], BF16, 1)
-            nc.gpsimd.tensor_tensor(out=h_grp[s][:, :hi, :], in0=mag[s][:, :, :hi].rearrange("p t c -> p c t"),
-                                    in1=wave[s][:, :, :hi].rearrange("p t c -> p c t"), op=ALU.mult)
 
         def quantize_h(s, lo, hi):
             if lo == 0:
@@ -332,40 +327,36 @@ def tile_banded_cosine_vocoder_head_k7_kernel(
         sort_w_codes(1, LOGMAG)
         write_all(weave(phases(0)[:2], magnitudes(0)[2:]))
         quantize_x(1)
-        write_all(weave(magnitudes(1) + magnitudes(2) + magnitudes(3), phases(0)[2:] + [(sort_w_codes, 1, PHASE)] + phases(1)))
+        write_all(weave(magnitudes(1) + magnitudes(2), phases(0)[2:] + [(sort_w_codes, 1, PHASE)] + phases(1)))
         write_all(cosines(0) + cosines(1))
-        for u in range(2, G):
-            sort_w_scale(u)
-            sort_w_codes(u, LOGMAG)
-        sort_w_codes(2, PHASE)
+        sort_w_scale(2)
+        sort_w_codes(2, LOGMAG)
 
         last = STEPS - 1
+        late_sorts = {1: [(sort_w_codes, 2, PHASE)], 2: [(sort_w_scale, 3), (sort_w_codes, 3, LOGMAG)], 3: [(sort_w_codes, 3, PHASE)]}
 
-        def sbuf_work(s, lo):
-            make_h(s - 1, lo, FR)
-            if s == 1:
-                sort_w_codes(3, PHASE)
+        def sbuf_work(s):
+            make_h(s - 1, 0, FR)
+            if s <= 3:
+                write_all(late_sorts[s])
             if s >= 4:
                 quantize_y(s - 4, 0, FR)
             quantize_h(s - 1, 0, FR)
 
-        sbuf_work(1, 0)
+        sbuf_work(1)
         for s in range(2, STEPS):
-            share = SHARES[s]
-            if share:
-                make_h_share(s - 1, share)
             if s == 2:
                 own = phases(s)[:3] + weave(finishes(groups_of(s)), phases(s)[3:])
             else:
                 own = weave(finishes(groups_of(s)), phases(s))
-            if s in (2, 4):
-                write_all(weave(own, magnitudes(s + 2) + magnitudes(s + 3)))
+            if s in AHEAD:
+                write_all(weave(own, [task for a in AHEAD[s] for task in magnitudes(a)]))
                 write_all(roundings(groups_of(s)) + cosines(s))
             else:
                 write_all(own)
                 write_all(weave(roundings(groups_of(s)), cosines(s)))
             write_all(turnings(groups_of(s)))
-            sbuf_work(s, share)
+            sbuf_work(s)
 
         synth_free.extend(["phase"] * BANKS["phase"])
         synthesize_next()

@@ -24,7 +24,8 @@ STEPS = G * T // FR
 LOGMAG, PHASE = 0, 1
 INV_2PI = 1.0 / (2.0 * math.pi)
 BANKS = {"phase": 3, "synth": 2, "side": 3}
-AHEAD = {2: (3, 4, 5), 4: (6, 7)}
+AHEAD = {2: (4, 5), 5: (6, 7)}
+SHARES = {1: 256, 3: 96, 4: 96, 6: 96}
 QUARTER = 0.25 + 2.0 ** -25
 
 
@@ -48,7 +49,8 @@ def tile_banded_cosine_vocoder_head_k7_kernel(
             return psum.tile([P, 512], F32, name=tag, tag=tag, bufs=BANKS[tag])
 
         amp_raw = kept("amp_raw", [P, G, PACK], BF16)
-        ws_raw = kept("ws_raw", [P, G, 2 * F], U8)
+        ws_raw = kept("ws_raw", [P, 2 * F], U8)
+        w_scale = [kept("w_scale%d" % u, [P, 2 * F], U8) for u in range(G)]
         wc_raw = [kept("wc_raw%d" % u, [P, 4 * F], U8) for u in range(G)]
         x_raw = [[kept("x_raw%d%d" % (hf, g), [P, 2, C], BF16) for g in range(2)] for hf in range(2)]
         b_codes = kept("b_codes", [P, G, 2 * N], U8)
@@ -57,8 +59,10 @@ def tile_banded_cosine_vocoder_head_k7_kernel(
         r_sb = [kept("r_sb%d" % s, [P, 2, 2, N], BF16) for s in range(STEPS)]
         ident = kept("ident", [P, P], F32)
 
-        nc.vector.memset(ws_raw[:].rearrange("p u n -> p (u n)").bitcast(I32), 0)
+        nc.vector.memset(ws_raw[:].bitcast(I32), 0)
         make_identity(nc, ident[:])
+        for u in range(1, G):
+            nc.gpsimd.memset(w_scale[u][:].bitcast(I32), 0)
         nc.gpsimd.memset(b_scale[:].rearrange("p u n -> p (u n)").bitcast(I32), 0)
 
         def frames_of(dram, hf):
@@ -73,16 +77,14 @@ def tile_banded_cosine_vocoder_head_k7_kernel(
         for g in range(2):
             nc.sync.dma_start(out=x_raw[0][g][:], in_=frames_of(x, 0)[:, g, :, :])
         nc.sync.dma_start(out=wc_raw[0][:].bitcast(I32), in_=w_words[0].bitcast(I32))
-        load_scale_rows(ws_raw, w_scales)
+        for q in range(4):
+            nc.sync.dma_start(out=ws_raw[32 * q:32 * q + 4 * G, :].bitcast(I32), in_=w_scales[:, 4 * q:4 * q + 4, :].bitcast(I32))
         for g in range(2):
             nc.sync.dma_start(out=x_raw[1][g][:], in_=frames_of(x, 1)[:, g, :, :])
         for u in range(1, G):
             nc.sync.dma_start(out=wc_raw[u][:].bitcast(I32), in_=w_words[u].bitcast(I32))
         load_scale_rows(b_scale, b_scales)
         nc.sync.dma_start(out=b_codes[:].bitcast(I32), in_=b_words.rearrange("u p n -> p u n").bitcast(I32))
-        nc.sync.dma_start(out=gain_all[:], in_=gain.rearrange("u n -> (u n)").partition_broadcast(P))
-        for s in range(STEPS):
-            nc.sync.dma_start(out=r_sb[s][:], in_=frames_of(r[s // 2], s % 2))
 
         amp32 = kept("amp32", [P, G * PACK], F32)
         mant = kept("mant", [P, G * PACK], I32)
@@ -107,16 +109,22 @@ def tile_banded_cosine_vocoder_head_k7_kernel(
         nc.gpsimd.tensor_tensor(out=log_amp[:], in0=mant_ln[:], in1=expo_ln[:], op=ALU.add)
 
         w_codes = [kept("w_codes%d" % u, [P, 2, 2 * F], U8) for u in range(G)]
-        w_scale = [kept("w_scale%d" % u, [P, 2, F], U8) for u in range(G)]
-
-        def sort_w_scale(u):
-            nc.vector.tensor_copy(out=w_scale[u][:].rearrange("p h (t c i) -> p h c t i", t=PACK, i=16),
-                                  in_=ws_raw[:, u, :].rearrange("p (h c i t) -> p h c t i", h=2, t=PACK, i=16))
 
         def sort_w_codes(u, half):
             nc.vector.tensor_copy(
                 out=w_codes[u][:, half, :].rearrange("p (t c i b) -> p c t i b", t=PACK, i=8, b=2),
                 in_=wc_raw[u][:, half * 2 * F:(half + 1) * 2 * F].rearrange("p (c i t b) -> p c t i b", t=PACK, i=8, b=2))
+
+        def spread_w_scales():
+            nc.vector.tensor_copy(out=w_scale[0][:].rearrange("p (h t c i) -> p h c t i", h=2, t=PACK, i=16),
+                                  in_=ws_raw[:].rearrange("p (h c i t) -> p h c t i", h=2, t=PACK, i=16))
+            for u in range(1, G):
+                for q in range(4):
+                    nc.sync.dma_start(out=w_scale[u][32 * q:32 * q + 4, :].bitcast(I32),
+                                      in_=w_scale[0][32 * q + 4 * u:32 * q + 4 * u + 4, :].bitcast(I32))
+            nc.sync.dma_start(out=gain_all[:], in_=gain.rearrange("u n -> (u n)").partition_broadcast(P))
+            for s in range(STEPS):
+                nc.sync.dma_start(out=r_sb[s][:], in_=frames_of(r[s // 2], s % 2))
 
         x_grp = [kept("x_grp%d" % hf, [P, FR * PACK], BF16) for hf in range(2)]
         x_codes = [kept("x_codes%d" % hf, [P, FR], U32) for hf in range(2)]
@@ -131,9 +139,9 @@ def tile_banded_cosine_vocoder_head_k7_kernel(
                     nc.tensor.transpose(tv[:, j, u, :], words[:, u:256:2], ident[:])
             return tv
 
-        def group_x(hf, g, tv, copy):
+        def group_x(hf, g, tv):
             dst = x_grp[hf][:, 1024 * g:1024 * (g + 1)].bitcast(F32).rearrange("p (j r u) -> p j r u", j=2, u=2)
-            copy(out=dst, in_=tv.rearrange("p j u r -> p j r u"))
+            nc.scalar.copy(out=dst, in_=tv.rearrange("p j u r -> p j r u"))
 
         def quantize_x(hf):
             nc.vector.quantize_mx(out=x_codes[hf][:].bitcast(FP8X4), scales=x_scale[hf][:], in_=x_grp[hf][:])
@@ -142,7 +150,7 @@ def tile_banded_cosine_vocoder_head_k7_kernel(
             u, hf = divmod(s, 2)
             zb = bank(tag)
             nc.tensor.matmul_mx(out=zb[:], lhsT=w_codes[u][:, half, 256 * t:256 * (t + 1)].bitcast(FP4X4),
-                                lhsT_scale=w_scale[u][:, half, P * t:P * (t + 1)],
+                                lhsT_scale=w_scale[u][:, half * F + P * t:half * F + P * (t + 1)],
                                 rhs=x_codes[hf][:].bitcast(FP8X4), rhs_scale=x_scale[hf][:], start=True, stop=True)
             return zb
 
@@ -184,11 +192,22 @@ def tile_banded_cosine_vocoder_head_k7_kernel(
         h_grp = {}
 
         def make_h(s, lo, hi):
-            if lo == 0:
+            if s not in h_grp:
                 h_grp[s] = rotating("h_grp", [P, FR, PACK], BF16, 1)
             nc.vector.tensor_tensor(out=h_grp[s][:, lo:hi, :].rearrange("p (c i) t -> p c t i", i=4),
                                     in0=mag[s][:, :, lo:hi].rearrange("p t (c i) -> p c t i", i=4),
                                     in1=wave[s][:, :, lo:hi].rearrange("p t (c i) -> p c t i", i=4), op=ALU.mult)
+
+        def parked(s, share):
+            return h_grp[s][:, FR - share:, :].rearrange("p c t -> p (c t)").rearrange("p (t c) -> p t c", t=PACK)
+
+        def make_h_share(s, share):
+            h_grp[s] = rotating("h_grp", [P, FR, PACK], BF16, 1)
+            nc.gpsimd.tensor_tensor(out=parked(s, share), in0=mag[s][:, :, :share], in1=wave[s][:, :, :share], op=ALU.mult)
+
+        def group_h_share(s, share):
+            nc.scalar.copy(out=h_grp[s][:, :share, :].rearrange("p (c i) t -> p c t i", i=4),
+                           in_=parked(s, share).rearrange("p t (c i) -> p c t i", i=4))
 
         def quantize_h(s, lo, hi):
             if lo == 0:
@@ -263,16 +282,19 @@ def tile_banded_cosine_vocoder_head_k7_kernel(
 
         words_out = out_1[0].rearrange("p m t -> p (m t)")
 
-        def quantize_y(s, lo, hi):
-            y_codes = rotating("y_codes", [P, FR], U32, 4)
-            nc.vector.quantize_mx(out=y_codes[:, lo:hi].bitcast(FP8X4), scales=y_scale[:, FR * s + lo:FR * s + hi],
-                                  in_=y_grp[s][:, PACK * lo:PACK * hi])
-            nc.sync.dma_start(out=words_out[:, PACK * (FR * s + lo):PACK * (FR * s + hi)].bitcast(I32),
-                              in_=y_codes[:, lo:hi].bitcast(I32))
+        y_codes = {}
 
-        def store_scales(lo, hi):
+        def quantize_y(s, lo, hi):
+            if lo == 0:
+                y_codes[s] = rotating("y_codes", [P, FR], U32, 3)
+            nc.vector.quantize_mx(out=y_codes[s][:, lo:hi].bitcast(FP8X4), scales=y_scale[:, FR * s + lo:FR * s + hi],
+                                  in_=y_grp[s][:, PACK * lo:PACK * hi])
+            if hi == FR:
+                nc.sync.dma_start(out=words_out[:, PACK * FR * s:PACK * FR * (s + 1)].bitcast(I32), in_=y_codes[s][:].bitcast(I32))
+
+        def store_scales(lo, hi, queues):
             for q in range(4):
-                nc.sync.dma_start(out=out_2[0, 4 * q:4 * q + 4, lo:hi].bitcast(I32),
+                queues[q].dma_start(out=out_2[0, 4 * q:4 * q + 4, lo:hi].bitcast(I32),
                                   in_=y_scale[32 * q:32 * q + 4, lo:hi].bitcast(I32))
 
         def finish(s, jj):
@@ -308,59 +330,72 @@ def tile_banded_cosine_vocoder_head_k7_kernel(
 
         x00 = turn_x(0, 0)
         x01 = turn_x(0, 1)
-        group_x(0, 0, x00, nc.vector.tensor_copy)
-        sort_w_codes(0, LOGMAG)
-        group_x(0, 1, x01, nc.vector.tensor_copy)
+        group_x(0, 0, x00)
+        group_x(0, 1, x01)
         x10 = turn_x(1, 0)
         x11 = turn_x(1, 1)
-        sort_w_scale(0)
+        sort_w_codes(0, LOGMAG)
+        spread_w_scales()
         quantize_x(0)
         sort_w_codes(0, PHASE)
         magnitude(0, 0)
         project_next_phase()
-        group_x(1, 0, x10, nc.scalar.copy)
-        group_x(1, 1, x11, nc.scalar.copy)
+        group_x(1, 0, x10)
+        group_x(1, 1, x11)
         project_next_phase()
         magnitude(0, 1)
         project_next_phase()
-        sort_w_scale(1)
         sort_w_codes(1, LOGMAG)
+        sort_w_codes(1, PHASE)
         write_all(weave(phases(0)[:2], magnitudes(0)[2:]))
         quantize_x(1)
-        write_all(weave(magnitudes(1) + magnitudes(2), phases(0)[2:] + [(sort_w_codes, 1, PHASE)] + phases(1)))
+        write_all(weave(magnitudes(1) + magnitudes(2), phases(0)[2:] + phases(1)))
         write_all(cosines(0) + cosines(1))
-        sort_w_scale(2)
-        sort_w_codes(2, LOGMAG)
+        for u in range(2, G):
+            sort_w_codes(u, LOGMAG)
+            sort_w_codes(u, PHASE)
 
         last = STEPS - 1
-        late_sorts = {1: [(sort_w_codes, 2, PHASE)], 2: [(sort_w_scale, 3), (sort_w_codes, 3, LOGMAG)], 3: [(sort_w_codes, 3, PHASE)]}
 
         def sbuf_work(s):
-            make_h(s - 1, 0, FR)
-            if s <= 3:
-                write_all(late_sorts[s])
+            lo = SHARES.get(s - 1, 0)
             if s >= 4:
+                make_h(s - 1, lo, FR)
                 quantize_y(s - 4, 0, FR)
-            quantize_h(s - 1, 0, FR)
+                quantize_h(s - 1, 0, FR)
+            else:
+                if lo < FR // 2:
+                    make_h(s - 1, lo, FR // 2)
+                make_h(s - 1, FR // 2, FR)
+                quantize_h(s - 1, 0, FR // 2)
+                quantize_h(s - 1, FR // 2, FR)
 
+        write_all(magnitudes(3)[:3])
         sbuf_work(1)
         for s in range(2, STEPS):
+            share = SHARES.get(s - 1, 0)
+            grouping = [(group_h_share, s - 1, share)] if share else []
+            if share:
+                make_h_share(s - 1, share)
             if s == 2:
                 own = phases(s)[:3] + weave(finishes(groups_of(s)), phases(s)[3:])
             else:
                 own = weave(finishes(groups_of(s)), phases(s))
             if s in AHEAD:
-                write_all(weave(own, [task for a in AHEAD[s] for task in magnitudes(a)]))
+                ahead = (magnitudes(3)[3:] if s == 2 else []) + [task for a in AHEAD[s] for task in magnitudes(a)]
+                write_all(weave(own, ahead[:PACK] + grouping + ahead[PACK:]))
                 write_all(roundings(groups_of(s)) + cosines(s))
             else:
                 write_all(own)
-                write_all(weave(roundings(groups_of(s)), cosines(s)))
-            write_all(turnings(groups_of(s)))
+                write_all(grouping + weave(roundings(groups_of(s)), cosines(s)))
+            if s != 2:
+                write_all(turnings((groups_of(2) if s == 3 else []) + groups_of(s)))
             sbuf_work(s)
 
         synth_free.extend(["phase"] * BANKS["phase"])
         synthesize_next()
         quantize_y(last - 3, 0, FR)
+        store_scales(0, FR * (last - 2), [nc.sync] * 4)
         make_h(last, 0, FR // 2)
         make_h(last, FR // 2, FR)
         quantize_h(last, 0, FR // 2)
@@ -375,12 +410,10 @@ def tile_banded_cosine_vocoder_head_k7_kernel(
                 apply_gain(s, jj, sums[s, jj], nc.vector)
             for jj in (2 * g, 2 * g + 1):
                 round_y(s, jj, nc.scalar.copy if s < last else nc.vector.tensor_copy)
-            if s < last:
-                quantize_y(last - 2, 0, FR)
-                store_scales(0, FR * (last - 1))
             turn_y(s, g)
             group_y(s, g)
+        quantize_y(last - 2, 0, FR)
         quantize_y(last - 1, 0, FR)
         quantize_y(last, 0, FR // 2)
         quantize_y(last, FR // 2, FR)
-        store_scales(FR * (last - 1), FR * STEPS)
+        store_scales(FR * (last - 2), FR * STEPS, [nc.scalar, nc.sync] * 2)

@@ -18,15 +18,20 @@ ALU = mybir.AluOpType
 ACT = mybir.ActivationFunctionType
 
 P = 128
-PACK = 4
-FR = 512
-STEPS = G * T // FR
+SLOTS = 4
+QUADRANTS = 4
+FRAMES = 512
+GROUP = 256
+STEPS = G * T // FRAMES
+LAST = STEPS - 1
 LOGMAG, PHASE = 0, 1
 INV_2PI = 1.0 / (2.0 * math.pi)
+QUARTER_TURN = 0.25 + 2.0 ** -25
+
 BANKS = {"phase": 3, "synth": 2, "side": 3}
-AHEAD = {2: (4, 5), 5: (6, 7)}
-SHARES = {1: 256, 3: 96, 4: 96, 6: 96}
-QUARTER = 0.25 + 2.0 ** -25
+EARLY_EXP, LATE_EXP = 2, 5
+MAG_TILES = 5
+H_SHARE = 96
 
 
 def tile_banded_cosine_vocoder_head_k7_kernel(
@@ -48,11 +53,14 @@ def tile_banded_cosine_vocoder_head_k7_kernel(
         def bank(tag):
             return psum.tile([P, 512], F32, name=tag, tag=tag, bufs=BANKS[tag])
 
-        amp_raw = kept("amp_raw", [P, G, PACK], BF16)
+        def by_tile(rows, half):
+            return rows[half * FRAMES:(half + 1) * FRAMES, :].rearrange("(g p j) c -> p g j c", g=2, j=2)
+
+        amp_raw = kept("amp_raw", [P, G, SLOTS], BF16)
         ws_raw = kept("ws_raw", [P, 2 * F], U8)
         w_scale = [kept("w_scale%d" % u, [P, 2 * F], U8) for u in range(G)]
         wc_raw = [kept("wc_raw%d" % u, [P, 4 * F], U8) for u in range(G)]
-        x_raw = [[kept("x_raw%d%d" % (hf, g), [P, 2, C], BF16) for g in range(2)] for hf in range(2)]
+        x_raw = [[kept("x_raw%d%d" % (half, g), [P, 2, C], BF16) for g in range(2)] for half in range(2)]
         b_codes = kept("b_codes", [P, G, 2 * N], U8)
         b_scale = kept("b_scale", [P, G, N], U8)
         gain_all = kept("gain_all", [P, G * N], BF16)
@@ -65,36 +73,30 @@ def tile_banded_cosine_vocoder_head_k7_kernel(
             nc.gpsimd.memset(w_scale[u][:].bitcast(I32), 0)
         nc.gpsimd.memset(b_scale[:].rearrange("p u n -> p (u n)").bitcast(I32), 0)
 
-        def frames_of(dram, hf):
-            return dram[hf * FR:(hf + 1) * FR, :].rearrange("(g p j) c -> p g j c", g=2, j=2)
-
-        def load_scale_rows(plane, rows):
-            for q in range(4):
-                nc.sync.dma_start(out=plane[32 * q:32 * q + 4, :, :].bitcast(I32),
-                                  in_=rows[:, 4 * q:4 * q + 4, :].rearrange("u r n -> r u n").bitcast(I32))
-
-        nc.sync.dma_start(out=amp_raw[:], in_=amp.rearrange("u (p t) -> p u t", t=PACK))
-        for g in range(2):
-            nc.sync.dma_start(out=x_raw[0][g][:], in_=frames_of(x, 0)[:, g, :, :])
-        nc.sync.dma_start(out=wc_raw[0][:].bitcast(I32), in_=w_words[0].bitcast(I32))
-        for q in range(4):
+        nc.scalar.dma_start(out=amp_raw[:], in_=amp.rearrange("u (p t) -> p u t", t=SLOTS))
+        nc.sync.dma_start(out=x_raw[0][0][:], in_=by_tile(x, 0)[:, 0, :, :])
+        for q in range(QUADRANTS):
             nc.sync.dma_start(out=ws_raw[32 * q:32 * q + 4 * G, :].bitcast(I32), in_=w_scales[:, 4 * q:4 * q + 4, :].bitcast(I32))
+        nc.sync.dma_start(out=x_raw[0][1][:], in_=by_tile(x, 0)[:, 1, :, :])
+        nc.sync.dma_start(out=wc_raw[0][:].bitcast(I32), in_=w_words[0].bitcast(I32))
         for g in range(2):
-            nc.sync.dma_start(out=x_raw[1][g][:], in_=frames_of(x, 1)[:, g, :, :])
+            nc.sync.dma_start(out=x_raw[1][g][:], in_=by_tile(x, 1)[:, g, :, :])
         for u in range(1, G):
             nc.sync.dma_start(out=wc_raw[u][:].bitcast(I32), in_=w_words[u].bitcast(I32))
-        load_scale_rows(b_scale, b_scales)
+        for q in range(QUADRANTS):
+            nc.sync.dma_start(out=b_scale[32 * q:32 * q + 4, :, :].bitcast(I32),
+                              in_=b_scales[:, 4 * q:4 * q + 4, :].rearrange("u i n -> i u n").bitcast(I32))
         nc.sync.dma_start(out=b_codes[:].bitcast(I32), in_=b_words.rearrange("u p n -> p u n").bitcast(I32))
 
-        amp32 = kept("amp32", [P, G * PACK], F32)
-        mant = kept("mant", [P, G * PACK], I32)
-        expo = kept("expo", [P, G * PACK], I32)
-        expo_ln = kept("expo_ln", [P, G * PACK], F32)
-        mant_ln = kept("mant_ln", [P, G * PACK], F32)
-        log_amp = kept("log_amp", [P, G * PACK], F32)
-        sgn = kept("sgn", [P, G * PACK], F32)
-        sin_scale = kept("sin_scale", [P, G * PACK], F32)
-        sin_bias = kept("sin_bias", [P, G * PACK], F32)
+        amp32 = kept("amp32", [P, G * SLOTS], F32)
+        mant = kept("mant", [P, G * SLOTS], I32)
+        expo = kept("expo", [P, G * SLOTS], I32)
+        expo_ln = kept("expo_ln", [P, G * SLOTS], F32)
+        mant_ln = kept("mant_ln", [P, G * SLOTS], F32)
+        log_amp = kept("log_amp", [P, G * SLOTS], F32)
+        sgn = kept("sgn", [P, G * SLOTS], F32)
+        sin_scale = kept("sin_scale", [P, G * SLOTS], F32)
+        sin_bias = kept("sin_bias", [P, G * SLOTS], F32)
         nc.vector.tensor_copy(out=amp32[:], in_=amp_raw[:].rearrange("p u t -> p (u t)"))
         nc.vector.tensor_scalar(out=mant[:], in0=amp32[:].bitcast(I32), scalar1=0x007FFFFF, scalar2=0x3F800000,
                                 op0=ALU.bitwise_and, op1=ALU.bitwise_or)
@@ -110,62 +112,62 @@ def tile_banded_cosine_vocoder_head_k7_kernel(
 
         w_codes = [kept("w_codes%d" % u, [P, 2, 2 * F], U8) for u in range(G)]
 
-        def sort_w_codes(u, half):
+        def sort_w_codes(u, part):
             nc.vector.tensor_copy(
-                out=w_codes[u][:, half, :].rearrange("p (t c i b) -> p c t i b", t=PACK, i=8, b=2),
-                in_=wc_raw[u][:, half * 2 * F:(half + 1) * 2 * F].rearrange("p (c i t b) -> p c t i b", t=PACK, i=8, b=2))
+                out=w_codes[u][:, part, :].rearrange("p (t c i b) -> p c t i b", t=SLOTS, i=8, b=2),
+                in_=wc_raw[u][:, part * 2 * F:(part + 1) * 2 * F].rearrange("p (c i t b) -> p c t i b", t=SLOTS, i=8, b=2))
 
-        def spread_w_scales():
-            nc.vector.tensor_copy(out=w_scale[0][:].rearrange("p (h t c i) -> p h c t i", h=2, t=PACK, i=16),
-                                  in_=ws_raw[:].rearrange("p (h c i t) -> p h c t i", h=2, t=PACK, i=16))
+        def sort_w_scales():
+            nc.vector.tensor_copy(out=w_scale[0][:].rearrange("p (a t c i) -> p a c t i", a=2, t=SLOTS, i=16),
+                                  in_=ws_raw[:].rearrange("p (a c i t) -> p a c t i", a=2, t=SLOTS, i=16))
             for u in range(1, G):
-                for q in range(4):
+                for q in range(QUADRANTS):
                     nc.sync.dma_start(out=w_scale[u][32 * q:32 * q + 4, :].bitcast(I32),
                                       in_=w_scale[0][32 * q + 4 * u:32 * q + 4 * u + 4, :].bitcast(I32))
+
+        def preload_gain_and_r():
             nc.sync.dma_start(out=gain_all[:], in_=gain.rearrange("u n -> (u n)").partition_broadcast(P))
             for s in range(STEPS):
-                nc.sync.dma_start(out=r_sb[s][:], in_=frames_of(r[s // 2], s % 2))
+                nc.sync.dma_start(out=r_sb[s][:], in_=by_tile(r[s // 2], s % 2))
 
-        x_grp = [kept("x_grp%d" % hf, [P, FR * PACK], BF16) for hf in range(2)]
-        x_codes = [kept("x_codes%d" % hf, [P, FR], U32) for hf in range(2)]
-        x_scale = [kept("x_scale%d" % hf, [P, FR], U8) for hf in range(2)]
+        x_grp = [kept("x_grp%d" % half, [P, FRAMES * SLOTS], BF16) for half in range(2)]
+        x_codes = [kept("x_codes%d" % half, [P, FRAMES], U32) for half in range(2)]
+        x_scale = [kept("x_scale%d" % half, [P, FRAMES], U8) for half in range(2)]
+        x_turned = {}
 
-        def turn_x(hf, g):
-            tb = bank("side")
-            tv = tb[:].rearrange("p (j u r) -> p j u r", j=2, u=2)
+        def turn_x(half, g):
+            turned = bank("side")
+            x_turned[half, g] = turned[:].rearrange("p (j w row) -> p j w row", j=2, w=2)
             for j in range(2):
-                words = x_raw[hf][g][:, j, :].bitcast(F32)
-                for u in range(2):
-                    nc.tensor.transpose(tv[:, j, u, :], words[:, u:256:2], ident[:])
-            return tv
+                words = x_raw[half][g][:, j, :].bitcast(F32)
+                for w in range(2):
+                    nc.tensor.transpose(x_turned[half, g][:, j, w, :], words[:, w:C // 2:2], ident[:])
 
-        def group_x(hf, g, tv):
-            dst = x_grp[hf][:, 1024 * g:1024 * (g + 1)].bitcast(F32).rearrange("p (j r u) -> p j r u", j=2, u=2)
-            nc.scalar.copy(out=dst, in_=tv.rearrange("p j u r -> p j r u"))
+        def group_x(half, g):
+            words = x_grp[half][:, SLOTS * GROUP * g:SLOTS * GROUP * (g + 1)].bitcast(F32)
+            nc.scalar.copy(out=words.rearrange("p (j row w) -> p j row w", j=2, w=2),
+                           in_=x_turned[half, g].rearrange("p j w row -> p j row w"))
 
-        def quantize_x(hf):
-            nc.vector.quantize_mx(out=x_codes[hf][:].bitcast(FP8X4), scales=x_scale[hf][:], in_=x_grp[hf][:])
+        def quantize_x(half):
+            nc.vector.quantize_mx(out=x_codes[half][:].bitcast(FP8X4), scales=x_scale[half][:], in_=x_grp[half][:])
 
-        def project(s, half, t, tag):
-            u, hf = divmod(s, 2)
-            zb = bank(tag)
-            nc.tensor.matmul_mx(out=zb[:], lhsT=w_codes[u][:, half, 256 * t:256 * (t + 1)].bitcast(FP4X4),
-                                lhsT_scale=w_scale[u][:, half * F + P * t:half * F + P * (t + 1)],
-                                rhs=x_codes[hf][:].bitcast(FP8X4), rhs_scale=x_scale[hf][:], start=True, stop=True)
-            return zb
+        mag, wave, whole, phase_bank, h_grp, h_codes, h_scale = {}, {}, {}, {}, {}, {}, {}
+        phase_todo = [(s, t) for s in range(STEPS) for t in range(SLOTS)]
 
-        mag, wave, hq, hs, y_sb, y_bf, y_grp = {}, {}, {}, {}, {}, {}, {}
-        y_scale = kept("y_scale", [P, G * T], U8)
+        def project(s, part, t, tag):
+            u, half = divmod(s, 2)
+            z = bank(tag)
+            nc.tensor.matmul_mx(out=z[:], lhsT=w_codes[u][:, part, 2 * P * t:2 * P * (t + 1)].bitcast(FP4X4),
+                                lhsT_scale=w_scale[u][:, part * F + P * t:part * F + P * (t + 1)],
+                                rhs=x_codes[half][:].bitcast(FP8X4), rhs_scale=x_scale[half][:], start=True, stop=True)
+            return z
 
         def magnitude(s, t):
             if t == 0:
-                mag[s] = rotating("mag", [P, PACK, FR], F32, 5)
-            zb = project(s, LOGMAG, t, "side")
-            col = PACK * (s // 2) + t
-            nc.scalar.activation(out=mag[s][:, t, :], in_=zb[:], func=ACT.Exp, bias=log_amp[:, col:col + 1])
-
-        phase_todo = [(s, t) for s in range(STEPS) for t in range(PACK)]
-        phase_bank, whole = {}, {}
+                mag[s] = rotating("mag", [P, SLOTS, FRAMES], F32, MAG_TILES)
+            z = project(s, LOGMAG, t, "side")
+            col = SLOTS * (s // 2) + t
+            nc.scalar.activation(out=mag[s][:, t, :], in_=z[:], func=ACT.Exp, bias=log_amp[:, col:col + 1])
 
         def project_next_phase():
             if phase_todo:
@@ -173,36 +175,37 @@ def tile_banded_cosine_vocoder_head_k7_kernel(
                 phase_bank[s, t] = project(s, PHASE, t, "phase")
 
         def count_turns(s, t):
-            whole[s, t] = rotating("whole", [P, FR], I32, 3)
-            nc.vector.tensor_scalar(out=whole[s, t][:], in0=phase_bank[s, t][:], scalar1=INV_2PI, scalar2=QUARTER,
+            whole[s, t] = rotating("whole", [P, FRAMES], I32, BANKS["phase"])
+            nc.vector.tensor_scalar(out=whole[s, t][:], in0=phase_bank[s, t][:], scalar1=INV_2PI, scalar2=QUARTER_TURN,
                                     op0=ALU.mult, op1=ALU.add)
 
         def reduce_phase(s, t):
             if t == 0:
-                wave[s] = rotating("wave", [P, PACK, FR], F32, 2)
-            nc.vector.scalar_tensor_tensor(out=wave[s][:, t, :], in0=phase_bank[s, t][:], scalar=INV_2PI, in1=whole[s, t][:],
-                                           op0=ALU.mult, op1=ALU.subtract)
+                wave[s] = rotating("wave", [P, SLOTS, FRAMES], F32, 2)
+            nc.vector.scalar_tensor_tensor(out=wave[s][:, t, :], in0=phase_bank[s, t][:], scalar=INV_2PI,
+                                           in1=whole[s, t][:], op0=ALU.mult, op1=ALU.subtract)
             project_next_phase()
 
         def cosine(s, t):
-            col = PACK * (s // 2) + t
+            col = SLOTS * (s // 2) + t
             nc.scalar.activation(out=wave[s][:, t, :], in_=wave[s][:, t, :], func=ACT.Sin,
                                  scale=sin_scale[:, col:col + 1], bias=sin_bias[:, col:col + 1])
 
-        h_grp = {}
+        def new_h(s):
+            h_grp[s] = rotating("h_grp", [P, FRAMES, SLOTS], BF16, 1)
 
-        def make_h(s, lo, hi):
+        def multiply_h(s, lo, hi):
             if s not in h_grp:
-                h_grp[s] = rotating("h_grp", [P, FR, PACK], BF16, 1)
+                new_h(s)
             nc.vector.tensor_tensor(out=h_grp[s][:, lo:hi, :].rearrange("p (c i) t -> p c t i", i=4),
                                     in0=mag[s][:, :, lo:hi].rearrange("p t (c i) -> p c t i", i=4),
                                     in1=wave[s][:, :, lo:hi].rearrange("p t (c i) -> p c t i", i=4), op=ALU.mult)
 
         def parked(s, share):
-            return h_grp[s][:, FR - share:, :].rearrange("p c t -> p (c t)").rearrange("p (t c) -> p t c", t=PACK)
+            return h_grp[s][:, FRAMES - share:, :].rearrange("p c t -> p (c t)").rearrange("p (t c) -> p t c", t=SLOTS)
 
-        def make_h_share(s, share):
-            h_grp[s] = rotating("h_grp", [P, FR, PACK], BF16, 1)
+        def multiply_h_share(s, share):
+            new_h(s)
             nc.gpsimd.tensor_tensor(out=parked(s, share), in0=mag[s][:, :, :share], in1=wave[s][:, :, :share], op=ALU.mult)
 
         def group_h_share(s, share):
@@ -211,104 +214,109 @@ def tile_banded_cosine_vocoder_head_k7_kernel(
 
         def quantize_h(s, lo, hi):
             if lo == 0:
-                hq[s] = rotating("h_codes", [P, FR], U32, 3)
-                hs[s] = rotating("h_scale", [P, FR], U8, 3)
-            nc.vector.quantize_mx(out=hq[s][:, lo:hi].bitcast(FP8X4), scales=hs[s][:, lo:hi],
+                h_codes[s] = rotating("h_codes", [P, FRAMES], U32, 3)
+                h_scale[s] = rotating("h_scale", [P, FRAMES], U8, 3)
+            nc.vector.quantize_mx(out=h_codes[s][:, lo:hi].bitcast(FP8X4), scales=h_scale[s][:, lo:hi],
                                   in_=h_grp[s][:, lo:hi, :].rearrange("p c t -> p (c t)"))
-            synth_ready.extend((s, jj) for jj in range(lo // P, hi // P))
+            synth_ready.extend((s, tile) for tile in range(lo // P, hi // P))
             synthesize_next()
 
         synth_ready, synth_bank = [], {}
         synth_free = ["synth"] * BANKS["synth"]
+        y_sb, y_bf, y_turned, y_grp, y_codes = {}, {}, {}, {}, {}
+        y_scale = kept("y_scale", [P, G * T], U8)
+        words_out = out_1[0].rearrange("p m t -> p (m t)")
 
         def synthesize_next():
             while synth_ready and synth_free:
-                s, jj = synth_ready.pop(0)
+                s, tile = synth_ready.pop(0)
                 tag = synth_free.pop(0)
-                synth_bank[s, jj] = tag, bank(tag)
-                nc.tensor.matmul_mx(out=synth_bank[s, jj][1][:], lhsT=hq[s][:, P * jj:P * (jj + 1)].bitcast(FP8X4),
-                                    lhsT_scale=hs[s][:, P * jj:P * (jj + 1)],
+                synth_bank[s, tile] = tag, bank(tag)
+                nc.tensor.matmul_mx(out=synth_bank[s, tile][1][:], lhsT=h_codes[s][:, P * tile:P * (tile + 1)].bitcast(FP8X4),
+                                    lhsT_scale=h_scale[s][:, P * tile:P * (tile + 1)],
                                     rhs=b_codes[:, s // 2, :].bitcast(FP4X4), rhs_scale=b_scale[:, s // 2, :],
                                     start=True, stop=True)
 
-        def add_residual(s, jj):
-            g, j = divmod(jj, 2)
+        def add_residual(s, tile):
+            g, j = divmod(tile, 2)
             summed = rotating("summed", [P, N], F32, 8)
-            tag, ob = synth_bank.pop((s, jj))
-            nc.vector.tensor_tensor(out=summed[:], in0=ob[:], in1=r_sb[s][:, g, j, :], op=ALU.add)
+            tag, product = synth_bank.pop((s, tile))
+            nc.vector.tensor_tensor(out=summed[:], in0=product[:], in1=r_sb[s][:, g, j, :], op=ALU.add)
             synth_free.append(tag)
             synthesize_next()
             return summed
 
-        def apply_gain(s, jj, summed, engine):
-            u, hf = divmod(s, 2)
-            g, j = divmod(jj, 2)
-            if jj == 0:
+        def apply_gain(s, tile, summed, engine):
+            u, half = divmod(s, 2)
+            g, j = divmod(tile, 2)
+            if tile == 0:
                 y_sb[s] = rotating("y_sb", [P, 2, 2, N], F32, 3)
             engine.tensor_tensor(out=y_sb[s][:, g, j, :], in0=summed[:], in1=gain_all[:, u * N:(u + 1) * N], op=ALU.mult)
             if j == 1:
-                nc.sync.dma_start(out=frames_of(out_0[u], hf)[:, g, :, :], in_=y_sb[s][:, g, :, :])
+                nc.sync.dma_start(out=by_tile(out_0[u], half)[:, g, :, :], in_=y_sb[s][:, g, :, :])
 
-        def round_y(s, jj, copy):
-            g, j = divmod(jj, 2)
-            if jj == 0:
+        def finish(s, tile):
+            apply_gain(s, tile, add_residual(s, tile), nc.gpsimd)
+
+        def round_y(s, tile, copy):
+            g, j = divmod(tile, 2)
+            if tile == 0:
                 y_bf[s] = rotating("y_bf", [P, 4, N], BF16, 2)
-            copy(out=y_bf[s][:, jj, :].rearrange("p (u m e) -> p u m e", u=2, e=2),
-                 in_=y_sb[s][:, g, j, :].rearrange("p (m u e) -> p u m e", u=2, e=2))
-
-        turned = {}
+            copy(out=y_bf[s][:, tile, :].rearrange("p (w m e) -> p w m e", w=2, e=2),
+                 in_=y_sb[s][:, g, j, :].rearrange("p (m w e) -> p w m e", w=2, e=2))
 
         def turn_y(s, g):
-            tb = bank("side")
-            turned[s, g] = tb[:].rearrange("p (j u r) -> p j u r", j=2, u=2)
+            turned = bank("side")
+            y_turned[s, g] = turned[:].rearrange("p (j w row) -> p j w row", j=2, w=2)
             for j in range(2):
                 words = y_bf[s][:, 2 * g + j, :].bitcast(F32)
-                for u in range(2):
-                    nc.tensor.transpose(turned[s, g][:, j, u, :], words[:, P * u:P * (u + 1)], ident[:])
+                for w in range(2):
+                    nc.tensor.transpose(y_turned[s, g][:, j, w, :], words[:, P * w:P * (w + 1)], ident[:])
 
         def group_y(s, g):
             if g == 0:
-                y_grp[s] = rotating("y_grp", [P, FR * PACK], BF16, 3)
-            dst = y_grp[s][:, 1024 * g:1024 * (g + 1)].bitcast(F32).rearrange("p (r j u) -> p r j u", j=2, u=2)
-            nc.scalar.copy(out=dst, in_=turned[s, g].rearrange("p j u r -> p r j u"))
-
-        def magnitudes(s):
-            return [(magnitude, s, t) for t in range(PACK)]
-
-        def write(tasks, count):
-            for unused in range(min(count, len(tasks))):
-                call, *args = tasks.pop(0)
-                call(*args)
-
-        words_out = out_1[0].rearrange("p m t -> p (m t)")
-
-        y_codes = {}
+                y_grp[s] = rotating("y_grp", [P, FRAMES * SLOTS], BF16, 3)
+            words = y_grp[s][:, SLOTS * GROUP * g:SLOTS * GROUP * (g + 1)].bitcast(F32)
+            nc.scalar.copy(out=words.rearrange("p (row j w) -> p row j w", j=2, w=2),
+                           in_=y_turned[s, g].rearrange("p j w row -> p row j w"))
 
         def quantize_y(s, lo, hi):
             if lo == 0:
-                y_codes[s] = rotating("y_codes", [P, FR], U32, 3)
-            nc.vector.quantize_mx(out=y_codes[s][:, lo:hi].bitcast(FP8X4), scales=y_scale[:, FR * s + lo:FR * s + hi],
-                                  in_=y_grp[s][:, PACK * lo:PACK * hi])
-            if hi == FR:
-                nc.sync.dma_start(out=words_out[:, PACK * FR * s:PACK * FR * (s + 1)].bitcast(I32), in_=y_codes[s][:].bitcast(I32))
+                y_codes[s] = rotating("y_codes", [P, FRAMES], U32, 3)
+            nc.vector.quantize_mx(out=y_codes[s][:, lo:hi].bitcast(FP8X4), scales=y_scale[:, FRAMES * s + lo:FRAMES * s + hi],
+                                  in_=y_grp[s][:, SLOTS * lo:SLOTS * hi])
+            if hi == FRAMES:
+                nc.sync.dma_start(out=words_out[:, SLOTS * FRAMES * s:SLOTS * FRAMES * (s + 1)].bitcast(I32),
+                                  in_=y_codes[s][:].bitcast(I32))
 
-        def store_scales(lo, hi, queues):
-            for q in range(4):
-                queues[q].dma_start(out=out_2[0, 4 * q:4 * q + 4, lo:hi].bitcast(I32),
-                                  in_=y_scale[32 * q:32 * q + 4, lo:hi].bitcast(I32))
+        def store_scales(first, end, queues):
+            cols = slice(FRAMES * first, FRAMES * end)
+            for q in range(QUADRANTS):
+                queues[q].dma_start(out=out_2[0, 4 * q:4 * q + 4, cols].bitcast(I32),
+                                    in_=y_scale[32 * q:32 * q + 4, cols].bitcast(I32))
 
-        def finish(s, jj):
-            apply_gain(s, jj, add_residual(s, jj), nc.gpsimd)
+        def write(calls):
+            for call, *args in calls:
+                call(*args)
+
+        def weave(first, second):
+            woven = []
+            for n in range(max(len(first), len(second))):
+                woven.extend(first[n:n + 1] + second[n:n + 1])
+            return woven
 
         def phases(s):
             return [(count_turns, s, 0), (count_turns, s, 1), (reduce_phase, s, 0), (count_turns, s, 2),
                     (reduce_phase, s, 1), (count_turns, s, 3), (reduce_phase, s, 2), (reduce_phase, s, 3)]
 
-        def finishes(groups):
-            return [(finish, s, 2 * g + j) for s, g in groups for j in range(2)]
+        def magnitudes(*steps):
+            return [(magnitude, s, t) for s in steps for t in range(SLOTS)]
 
         def cosines(s):
-            return [(cosine, s, t) for t in range(PACK)]
+            return [(cosine, s, t) for t in range(SLOTS)]
+
+        def finishes(groups):
+            return [(finish, s, 2 * g + j) for s, g in groups for j in range(2)]
 
         def roundings(groups):
             return [(round_y, s, 2 * g + j, nc.scalar.copy) for s, g in groups for j in range(2)]
@@ -317,103 +325,99 @@ def tile_banded_cosine_vocoder_head_k7_kernel(
             return [(turn_y, s, g) for s, g in groups] + [(group_y, s, g) for s, g in groups]
 
         def groups_of(s):
-            return [divmod(n, 2) for n in (2 * s - 5, 2 * s - 4) if n >= 0]
+            return [(s - 3, 1), (s - 2, 0)] if s >= 3 else [(s - 2, 0)]
 
-        def weave(first, second):
-            woven = []
-            for n in range(max(len(first), len(second))):
-                woven.extend(first[n:n + 1] + second[n:n + 1])
-            return woven
+        def share_of(s):
+            if s in (0, EARLY_EXP, LATE_EXP):
+                return 0
+            if len(groups_of(s + 1)) == 1:
+                return GROUP
+            return H_SHARE
 
-        def write_all(tasks):
-            write(tasks, len(tasks))
+        def sbuf_work(s):
+            lo = share_of(s - 1)
+            if s >= 4:
+                multiply_h(s - 1, lo, FRAMES)
+                quantize_y(s - 4, 0, FRAMES)
+                quantize_h(s - 1, 0, FRAMES)
+            else:
+                if lo < GROUP:
+                    multiply_h(s - 1, lo, GROUP)
+                multiply_h(s - 1, GROUP, FRAMES)
+                quantize_h(s - 1, 0, GROUP)
+                quantize_h(s - 1, GROUP, FRAMES)
 
-        x00 = turn_x(0, 0)
-        x01 = turn_x(0, 1)
-        group_x(0, 0, x00)
-        group_x(0, 1, x01)
-        x10 = turn_x(1, 0)
-        x11 = turn_x(1, 1)
+        write([(turn_x, 0, 0), (turn_x, 0, 1), (group_x, 0, 0), (group_x, 0, 1), (turn_x, 1, 0), (turn_x, 1, 1)])
+        sort_w_scales()
+        preload_gain_and_r()
         sort_w_codes(0, LOGMAG)
-        spread_w_scales()
         quantize_x(0)
         sort_w_codes(0, PHASE)
         magnitude(0, 0)
         project_next_phase()
-        group_x(1, 0, x10)
-        group_x(1, 1, x11)
+        group_x(1, 0)
+        group_x(1, 1)
         project_next_phase()
         magnitude(0, 1)
         project_next_phase()
         sort_w_codes(1, LOGMAG)
         sort_w_codes(1, PHASE)
-        write_all(weave(phases(0)[:2], magnitudes(0)[2:]))
+        write(weave(phases(0)[:2], magnitudes(0)[2:]))
         quantize_x(1)
-        write_all(weave(magnitudes(1) + magnitudes(2), phases(0)[2:] + phases(1)))
-        write_all(cosines(0) + cosines(1))
+        write(weave(magnitudes(1, 2), phases(0)[2:] + phases(1)))
+        write(cosines(0) + cosines(1))
         for u in range(2, G):
             sort_w_codes(u, LOGMAG)
             sort_w_codes(u, PHASE)
-
-        last = STEPS - 1
-
-        def sbuf_work(s):
-            lo = SHARES.get(s - 1, 0)
-            if s >= 4:
-                make_h(s - 1, lo, FR)
-                quantize_y(s - 4, 0, FR)
-                quantize_h(s - 1, 0, FR)
-            else:
-                if lo < FR // 2:
-                    make_h(s - 1, lo, FR // 2)
-                make_h(s - 1, FR // 2, FR)
-                quantize_h(s - 1, 0, FR // 2)
-                quantize_h(s - 1, FR // 2, FR)
-
-        write_all(magnitudes(3)[:3])
+        early = magnitudes(3, 4, 5)
+        write(early[:BANKS["side"]])
         sbuf_work(1)
+
+        exps = {EARLY_EXP: early[BANKS["side"]:], LATE_EXP: magnitudes(6, 7)}
+        to_turn = []
         for s in range(2, STEPS):
-            share = SHARES.get(s - 1, 0)
-            grouping = [(group_h_share, s - 1, share)] if share else []
+            groups = groups_of(s)
+            share = share_of(s - 1)
+            regroup = [(group_h_share, s - 1, share)] if share else []
             if share:
-                make_h_share(s - 1, share)
-            if s == 2:
-                own = phases(s)[:3] + weave(finishes(groups_of(s)), phases(s)[3:])
+                multiply_h_share(s - 1, share)
+            if len(groups) == 1:
+                reads = phases(s)[:3] + weave(finishes(groups), phases(s)[3:])
             else:
-                own = weave(finishes(groups_of(s)), phases(s))
-            if s in AHEAD:
-                ahead = (magnitudes(3)[3:] if s == 2 else []) + [task for a in AHEAD[s] for task in magnitudes(a)]
-                write_all(weave(own, ahead[:PACK] + grouping + ahead[PACK:]))
-                write_all(roundings(groups_of(s)) + cosines(s))
+                reads = weave(finishes(groups), phases(s))
+            if s in exps:
+                write(weave(reads, exps[s][:SLOTS] + regroup + exps[s][SLOTS:]))
+                write(roundings(groups) + cosines(s))
             else:
-                write_all(own)
-                write_all(grouping + weave(roundings(groups_of(s)), cosines(s)))
-            if s != 2:
-                write_all(turnings((groups_of(2) if s == 3 else []) + groups_of(s)))
+                write(reads)
+                write(regroup + weave(cosines(s), roundings(groups)))
+            to_turn.extend(groups)
+            if s != EARLY_EXP:
+                write(turnings(to_turn))
+                to_turn.clear()
             sbuf_work(s)
 
         synth_free.extend(["phase"] * BANKS["phase"])
         synthesize_next()
-        quantize_y(last - 3, 0, FR)
-        store_scales(0, FR * (last - 2), [nc.sync] * 4)
-        make_h(last, 0, FR // 2)
-        make_h(last, FR // 2, FR)
-        quantize_h(last, 0, FR // 2)
-        quantize_h(last, FR // 2, FR)
-        on_gpsimd = [(last - 2, 1), (last - 1, 0)]
-        on_vector = [(last - 1, 1), (last, 0), (last, 1)]
-        write_all(finishes(on_gpsimd))
-        sums = {(s, jj): add_residual(s, jj) for s, g in on_vector for jj in (2 * g, 2 * g + 1)}
-        write_all(roundings(on_gpsimd) + turnings(on_gpsimd))
+        quantize_y(LAST - 3, 0, FRAMES)
+        store_scales(0, LAST - 2, [nc.sync] * QUADRANTS)
+        multiply_h(LAST, 0, GROUP)
+        multiply_h(LAST, GROUP, FRAMES)
+        quantize_h(LAST, 0, GROUP)
+        quantize_h(LAST, GROUP, FRAMES)
+        on_gpsimd = groups_of(STEPS)
+        on_vector = [(LAST - 1, 1), (LAST, 0), (LAST, 1)]
+        write(finishes(on_gpsimd))
+        sums = {(s, tile): add_residual(s, tile) for s, g in on_vector for tile in (2 * g, 2 * g + 1)}
+        write(roundings(on_gpsimd) + turnings(on_gpsimd))
         for s, g in on_vector:
-            for jj in (2 * g, 2 * g + 1):
-                apply_gain(s, jj, sums[s, jj], nc.vector)
-            for jj in (2 * g, 2 * g + 1):
-                round_y(s, jj, nc.scalar.copy if s < last else nc.vector.tensor_copy)
-            turn_y(s, g)
-            group_y(s, g)
-        quantize_y(last - 2, 0, FR)
-        quantize_y(last - 1, 0, FR)
-        quantize_y(last, 0, FR // 2)
-        quantize_y(last, FR // 2, FR)
-        store_scales(FR * (last - 2), FR * STEPS, [nc.scalar, nc.sync] * 2)
+            for tile in (2 * g, 2 * g + 1):
+                apply_gain(s, tile, sums[s, tile], nc.vector)
+            for tile in (2 * g, 2 * g + 1):
+                round_y(s, tile, nc.vector.tensor_copy if s == LAST else nc.scalar.copy)
+            write(turnings([(s, g)]))
+        quantize_y(LAST - 2, 0, FRAMES)
+        quantize_y(LAST - 1, 0, FRAMES)
+        quantize_y(LAST, 0, GROUP)
+        quantize_y(LAST, GROUP, FRAMES)
+        store_scales(LAST - 2, STEPS, [nc.scalar, nc.sync, nc.scalar, nc.sync])

import math
from contextlib import ExitStack

import concourse.mybir as mybir
from concourse.masks import make_identity

G, T, C, F, N = 4, 1024, 512, 512, 512
FLOPS = 2 * G * T * C * 2 * F + 2 * G * T * F * N

F32 = mybir.dt.float32
BF16 = mybir.dt.bfloat16
I32 = mybir.dt.int32
U32 = mybir.dt.uint32
U8 = mybir.dt.uint8
FP8X4 = mybir.dt.float8_e4m3fn_x4
FP4X4 = mybir.dt.float4_e2m1fn_x4
ALU = mybir.AluOpType
ACT = mybir.ActivationFunctionType

P = 128
SLOTS = 4
QUADRANTS = 4
FRAMES = 512
GROUP = 256
STEPS = G * T // FRAMES
LAST = STEPS - 1
LOGMAG, PHASE = 0, 1
INV_2PI = 1.0 / (2.0 * math.pi)
QUARTER_TURN = 0.25 + 2.0 ** -25

BANKS = {"phase": 3, "synth": 2, "side": 3}
EARLY_EXP, LATE_EXP = 2, 5
MAG_TILES = 5
H_SHARE = 96


def tile_banded_cosine_vocoder_head_k7_kernel(
    tc, x, w_words, w_scales, amp, b_words, b_scales, r, gain, out_0, out_1, out_2
):
    nc = tc.nc
    with ExitStack() as ctx:
        keep = ctx.enter_context(tc.tile_pool(name="keep", bufs=1))
        work = ctx.enter_context(tc.tile_pool(name="work", bufs=2))
        psum = ctx.enter_context(tc.psum_pool(name="psum", bufs=1))
        ctx.enter_context(tc.manual_schedule())

        def kept(name, shape, dtype):
            return keep.tile(shape, dtype, name=name, tag=name, align_bytes=64)

        def rotating(tag, shape, dtype, bufs):
            return work.tile(shape, dtype, name=tag, tag=tag, bufs=bufs, align_bytes=64)

        def bank(tag):
            return psum.tile([P, 512], F32, name=tag, tag=tag, bufs=BANKS[tag])

        def by_tile(rows, half):
            return rows[half * FRAMES:(half + 1) * FRAMES, :].rearrange("(g p j) c -> p g j c", g=2, j=2)

        amp_raw = kept("amp_raw", [P, G, SLOTS], BF16)
        ws_raw = kept("ws_raw", [P, 2 * F], U8)
        w_scale = [kept("w_scale%d" % u, [P, 2 * F], U8) for u in range(G)]
        wc_raw = [kept("wc_raw%d" % u, [P, 4 * F], U8) for u in range(G)]
        x_raw = [[kept("x_raw%d%d" % (half, g), [P, 2, C], BF16) for g in range(2)] for half in range(2)]
        b_codes = kept("b_codes", [P, G, 2 * N], U8)
        b_scale = kept("b_scale", [P, G, N], U8)
        gain_all = kept("gain_all", [P, G * N], BF16)
        r_sb = [kept("r_sb%d" % s, [P, 2, 2, N], BF16) for s in range(STEPS)]
        ident = kept("ident", [P, P], F32)

        nc.vector.memset(ws_raw[:].bitcast(I32), 0)
        make_identity(nc, ident[:])
        for u in range(1, G):
            nc.gpsimd.memset(w_scale[u][:].bitcast(I32), 0)
        nc.gpsimd.memset(b_scale[:].rearrange("p u n -> p (u n)").bitcast(I32), 0)

        nc.scalar.dma_start(out=amp_raw[:], in_=amp.rearrange("u (p t) -> p u t", t=SLOTS))
        nc.sync.dma_start(out=x_raw[0][0][:], in_=by_tile(x, 0)[:, 0, :, :])
        for q in range(QUADRANTS):
            nc.sync.dma_start(out=ws_raw[32 * q:32 * q + 4 * G, :].bitcast(I32), in_=w_scales[:, 4 * q:4 * q + 4, :].bitcast(I32))
        nc.sync.dma_start(out=x_raw[0][1][:], in_=by_tile(x, 0)[:, 1, :, :])
        nc.sync.dma_start(out=wc_raw[0][:].bitcast(I32), in_=w_words[0].bitcast(I32))
        for g in range(2):
            nc.sync.dma_start(out=x_raw[1][g][:], in_=by_tile(x, 1)[:, g, :, :])
        for u in range(1, G):
            nc.sync.dma_start(out=wc_raw[u][:].bitcast(I32), in_=w_words[u].bitcast(I32))
        for q in range(QUADRANTS):
            nc.sync.dma_start(out=b_scale[32 * q:32 * q + 4, :, :].bitcast(I32),
                              in_=b_scales[:, 4 * q:4 * q + 4, :].rearrange("u i n -> i u n").bitcast(I32))
        nc.sync.dma_start(out=b_codes[:].bitcast(I32), in_=b_words.rearrange("u p n -> p u n").bitcast(I32))

        amp32 = kept("amp32", [P, G * SLOTS], F32)
        mant = kept("mant", [P, G * SLOTS], I32)
        expo = kept("expo", [P, G * SLOTS], I32)
        expo_ln = kept("expo_ln", [P, G * SLOTS], F32)
        mant_ln = kept("mant_ln", [P, G * SLOTS], F32)
        log_amp = kept("log_amp", [P, G * SLOTS], F32)
        sgn = kept("sgn", [P, G * SLOTS], F32)
        sin_scale = kept("sin_scale", [P, G * SLOTS], F32)
        sin_bias = kept("sin_bias", [P, G * SLOTS], F32)
        nc.vector.tensor_copy(out=amp32[:], in_=amp_raw[:].rearrange("p u t -> p (u t)"))
        nc.vector.tensor_scalar(out=mant[:], in0=amp32[:].bitcast(I32), scalar1=0x007FFFFF, scalar2=0x3F800000,
                                op0=ALU.bitwise_and, op1=ALU.bitwise_or)
        nc.vector.tensor_scalar(out=expo[:], in0=amp32[:].bitcast(I32), scalar1=23, scalar2=0xFF,
                                op0=ALU.logical_shift_right, op1=ALU.bitwise_and)
        nc.vector.tensor_scalar(out=expo_ln[:], in0=expo[:], scalar1=-127.0, scalar2=math.log(2.0),
                                op0=ALU.add, op1=ALU.mult)
        nc.scalar.activation(out=mant_ln[:], in_=mant[:].bitcast(F32), func=ACT.Ln)
        nc.scalar.activation(out=sgn[:], in_=amp32[:], func=ACT.Sign)
        nc.scalar.activation(out=sin_scale[:], in_=sgn[:], func=ACT.Copy, scale=2.0 * math.pi)
        nc.scalar.activation(out=sin_bias[:], in_=sgn[:], func=ACT.Copy, scale=0.5 * math.pi)
        nc.gpsimd.tensor_tensor(out=log_amp[:], in0=mant_ln[:], in1=expo_ln[:], op=ALU.add)

        w_codes = [kept("w_codes%d" % u, [P, 2, 2 * F], U8) for u in range(G)]

        def sort_w_codes(u, part):
            nc.vector.tensor_copy(
                out=w_codes[u][:, part, :].rearrange("p (t c i b) -> p c t i b", t=SLOTS, i=8, b=2),
                in_=wc_raw[u][:, part * 2 * F:(part + 1) * 2 * F].rearrange("p (c i t b) -> p c t i b", t=SLOTS, i=8, b=2))

        def sort_w_scales():
            nc.vector.tensor_copy(out=w_scale[0][:].rearrange("p (a t c i) -> p a c t i", a=2, t=SLOTS, i=16),
                                  in_=ws_raw[:].rearrange("p (a c i t) -> p a c t i", a=2, t=SLOTS, i=16))
            for u in range(1, G):
                for q in range(QUADRANTS):
                    nc.sync.dma_start(out=w_scale[u][32 * q:32 * q + 4, :].bitcast(I32),
                                      in_=w_scale[0][32 * q + 4 * u:32 * q + 4 * u + 4, :].bitcast(I32))

        def preload_gain_and_r():
            nc.sync.dma_start(out=gain_all[:], in_=gain.rearrange("u n -> (u n)").partition_broadcast(P))
            for s in range(STEPS):
                nc.sync.dma_start(out=r_sb[s][:], in_=by_tile(r[s // 2], s % 2))

        x_grp = [kept("x_grp%d" % half, [P, FRAMES * SLOTS], BF16) for half in range(2)]
        x_codes = [kept("x_codes%d" % half, [P, FRAMES], U32) for half in range(2)]
        x_scale = [kept("x_scale%d" % half, [P, FRAMES], U8) for half in range(2)]
        x_turned = {}

        def turn_x(half, g):
            turned = bank("side")
            x_turned[half, g] = turned[:].rearrange("p (j w row) -> p j w row", j=2, w=2)
            for j in range(2):
                words = x_raw[half][g][:, j, :].bitcast(F32)
                for w in range(2):
                    nc.tensor.transpose(x_turned[half, g][:, j, w, :], words[:, w:C // 2:2], ident[:])

        def group_x(half, g):
            words = x_grp[half][:, SLOTS * GROUP * g:SLOTS * GROUP * (g + 1)].bitcast(F32)
            nc.scalar.copy(out=words.rearrange("p (j row w) -> p j row w", j=2, w=2),
                           in_=x_turned[half, g].rearrange("p j w row -> p j row w"))

        def quantize_x(half):
            nc.vector.quantize_mx(out=x_codes[half][:].bitcast(FP8X4), scales=x_scale[half][:], in_=x_grp[half][:])

        mag, wave, whole, phase_bank, h_grp, h_codes, h_scale = {}, {}, {}, {}, {}, {}, {}
        phase_todo = [(s, t) for s in range(STEPS) for t in range(SLOTS)]

        def project(s, part, t, tag):
            u, half = divmod(s, 2)
            z = bank(tag)
            nc.tensor.matmul_mx(out=z[:], lhsT=w_codes[u][:, part, 2 * P * t:2 * P * (t + 1)].bitcast(FP4X4),
                                lhsT_scale=w_scale[u][:, part * F + P * t:part * F + P * (t + 1)],
                                rhs=x_codes[half][:].bitcast(FP8X4), rhs_scale=x_scale[half][:], start=True, stop=True)
            return z

        def magnitude(s, t):
            if t == 0:
                mag[s] = rotating("mag", [P, SLOTS, FRAMES], F32, MAG_TILES)
            z = project(s, LOGMAG, t, "side")
            col = SLOTS * (s // 2) + t
            nc.scalar.activation(out=mag[s][:, t, :], in_=z[:], func=ACT.Exp, bias=log_amp[:, col:col + 1])

        def project_next_phase():
            if phase_todo:
                s, t = phase_todo.pop(0)
                phase_bank[s, t] = project(s, PHASE, t, "phase")

        def count_turns(s, t):
            whole[s, t] = rotating("whole", [P, FRAMES], I32, BANKS["phase"])
            nc.vector.tensor_scalar(out=whole[s, t][:], in0=phase_bank[s, t][:], scalar1=INV_2PI, scalar2=QUARTER_TURN,
                                    op0=ALU.mult, op1=ALU.add)

        def reduce_phase(s, t):
            if t == 0:
                wave[s] = rotating("wave", [P, SLOTS, FRAMES], F32, 2)
            nc.vector.scalar_tensor_tensor(out=wave[s][:, t, :], in0=phase_bank[s, t][:], scalar=INV_2PI,
                                           in1=whole[s, t][:], op0=ALU.mult, op1=ALU.subtract)
            project_next_phase()

        def cosine(s, t):
            col = SLOTS * (s // 2) + t
            nc.scalar.activation(out=wave[s][:, t, :], in_=wave[s][:, t, :], func=ACT.Sin,
                                 scale=sin_scale[:, col:col + 1], bias=sin_bias[:, col:col + 1])

        def new_h(s):
            h_grp[s] = rotating("h_grp", [P, FRAMES, SLOTS], BF16, 1)

        def multiply_h(s, lo, hi):
            if s not in h_grp:
                new_h(s)
            nc.vector.tensor_tensor(out=h_grp[s][:, lo:hi, :].rearrange("p (c i) t -> p c t i", i=4),
                                    in0=mag[s][:, :, lo:hi].rearrange("p t (c i) -> p c t i", i=4),
                                    in1=wave[s][:, :, lo:hi].rearrange("p t (c i) -> p c t i", i=4), op=ALU.mult)

        def parked(s, share):
            return h_grp[s][:, FRAMES - share:, :].rearrange("p c t -> p (c t)").rearrange("p (t c) -> p t c", t=SLOTS)

        def multiply_h_share(s, share):
            new_h(s)
            nc.gpsimd.tensor_tensor(out=parked(s, share), in0=mag[s][:, :, :share], in1=wave[s][:, :, :share], op=ALU.mult)

        def group_h_share(s, share):
            nc.scalar.copy(out=h_grp[s][:, :share, :].rearrange("p (c i) t -> p c t i", i=4),
                           in_=parked(s, share).rearrange("p t (c i) -> p c t i", i=4))

        def quantize_h(s, lo, hi):
            if lo == 0:
                h_codes[s] = rotating("h_codes", [P, FRAMES], U32, 3)
                h_scale[s] = rotating("h_scale", [P, FRAMES], U8, 3)
            nc.vector.quantize_mx(out=h_codes[s][:, lo:hi].bitcast(FP8X4), scales=h_scale[s][:, lo:hi],
                                  in_=h_grp[s][:, lo:hi, :].rearrange("p c t -> p (c t)"))
            synth_ready.extend((s, tile) for tile in range(lo // P, hi // P))
            synthesize_next()

        synth_ready, synth_bank = [], {}
        synth_free = ["synth"] * BANKS["synth"]
        y_sb, y_bf, y_turned, y_grp, y_codes = {}, {}, {}, {}, {}
        y_scale = kept("y_scale", [P, G * T], U8)
        words_out = out_1[0].rearrange("p m t -> p (m t)")

        def synthesize_next():
            while synth_ready and synth_free:
                s, tile = synth_ready.pop(0)
                tag = synth_free.pop(0)
                synth_bank[s, tile] = tag, bank(tag)
                nc.tensor.matmul_mx(out=synth_bank[s, tile][1][:], lhsT=h_codes[s][:, P * tile:P * (tile + 1)].bitcast(FP8X4),
                                    lhsT_scale=h_scale[s][:, P * tile:P * (tile + 1)],
                                    rhs=b_codes[:, s // 2, :].bitcast(FP4X4), rhs_scale=b_scale[:, s // 2, :],
                                    start=True, stop=True)

        def add_residual(s, tile):
            g, j = divmod(tile, 2)
            summed = rotating("summed", [P, N], F32, 8)
            tag, product = synth_bank.pop((s, tile))
            nc.vector.tensor_tensor(out=summed[:], in0=product[:], in1=r_sb[s][:, g, j, :], op=ALU.add)
            synth_free.append(tag)
            synthesize_next()
            return summed

        def apply_gain(s, tile, summed, engine):
            u, half = divmod(s, 2)
            g, j = divmod(tile, 2)
            if tile == 0:
                y_sb[s] = rotating("y_sb", [P, 2, 2, N], F32, 3)
            engine.tensor_tensor(out=y_sb[s][:, g, j, :], in0=summed[:], in1=gain_all[:, u * N:(u + 1) * N], op=ALU.mult)
            if j == 1:
                nc.sync.dma_start(out=by_tile(out_0[u], half)[:, g, :, :], in_=y_sb[s][:, g, :, :])

        def finish(s, tile):
            apply_gain(s, tile, add_residual(s, tile), nc.gpsimd)

        def round_y(s, tile, copy):
            g, j = divmod(tile, 2)
            if tile == 0:
                y_bf[s] = rotating("y_bf", [P, 4, N], BF16, 2)
            copy(out=y_bf[s][:, tile, :].rearrange("p (w m e) -> p w m e", w=2, e=2),
                 in_=y_sb[s][:, g, j, :].rearrange("p (m w e) -> p w m e", w=2, e=2))

        def turn_y(s, g):
            turned = bank("side")
            y_turned[s, g] = turned[:].rearrange("p (j w row) -> p j w row", j=2, w=2)
            for j in range(2):
                words = y_bf[s][:, 2 * g + j, :].bitcast(F32)
                for w in range(2):
                    nc.tensor.transpose(y_turned[s, g][:, j, w, :], words[:, P * w:P * (w + 1)], ident[:])

        def group_y(s, g):
            if g == 0:
                y_grp[s] = rotating("y_grp", [P, FRAMES * SLOTS], BF16, 3)
            words = y_grp[s][:, SLOTS * GROUP * g:SLOTS * GROUP * (g + 1)].bitcast(F32)
            nc.scalar.copy(out=words.rearrange("p (row j w) -> p row j w", j=2, w=2),
                           in_=y_turned[s, g].rearrange("p j w row -> p row j w"))

        def quantize_y(s, lo, hi):
            if lo == 0:
                y_codes[s] = rotating("y_codes", [P, FRAMES], U32, 3)
            nc.vector.quantize_mx(out=y_codes[s][:, lo:hi].bitcast(FP8X4), scales=y_scale[:, FRAMES * s + lo:FRAMES * s + hi],
                                  in_=y_grp[s][:, SLOTS * lo:SLOTS * hi])
            if hi == FRAMES:
                nc.sync.dma_start(out=words_out[:, SLOTS * FRAMES * s:SLOTS * FRAMES * (s + 1)].bitcast(I32),
                                  in_=y_codes[s][:].bitcast(I32))

        def store_scales(first, end, queues):
            cols = slice(FRAMES * first, FRAMES * end)
            for q in range(QUADRANTS):
                queues[q].dma_start(out=out_2[0, 4 * q:4 * q + 4, cols].bitcast(I32),
                                    in_=y_scale[32 * q:32 * q + 4, cols].bitcast(I32))

        def write(calls):
            for call, *args in calls:
                call(*args)

        def weave(first, second):
            woven = []
            for n in range(max(len(first), len(second))):
                woven.extend(first[n:n + 1] + second[n:n + 1])
            return woven

        def phases(s):
            return [(count_turns, s, 0), (count_turns, s, 1), (reduce_phase, s, 0), (count_turns, s, 2),
                    (reduce_phase, s, 1), (count_turns, s, 3), (reduce_phase, s, 2), (reduce_phase, s, 3)]

        def magnitudes(*steps):
            return [(magnitude, s, t) for s in steps for t in range(SLOTS)]

        def cosines(s):
            return [(cosine, s, t) for t in range(SLOTS)]

        def finishes(groups):
            return [(finish, s, 2 * g + j) for s, g in groups for j in range(2)]

        def roundings(groups):
            return [(round_y, s, 2 * g + j, nc.scalar.copy) for s, g in groups for j in range(2)]

        def turnings(groups):
            return [(turn_y, s, g) for s, g in groups] + [(group_y, s, g) for s, g in groups]

        def groups_of(s):
            return [(s - 3, 1), (s - 2, 0)] if s >= 3 else [(s - 2, 0)]

        def share_of(s):
            if s in (0, EARLY_EXP, LATE_EXP):
                return 0
            if len(groups_of(s + 1)) == 1:
                return GROUP
            return H_SHARE

        def sbuf_work(s):
            lo = share_of(s - 1)
            if s >= 4:
                multiply_h(s - 1, lo, FRAMES)
                quantize_y(s - 4, 0, FRAMES)
                quantize_h(s - 1, 0, FRAMES)
            else:
                if lo < GROUP:
                    multiply_h(s - 1, lo, GROUP)
                multiply_h(s - 1, GROUP, FRAMES)
                quantize_h(s - 1, 0, GROUP)
                quantize_h(s - 1, GROUP, FRAMES)

        write([(turn_x, 0, 0), (turn_x, 0, 1), (group_x, 0, 0), (group_x, 0, 1), (turn_x, 1, 0), (turn_x, 1, 1)])
        sort_w_scales()
        preload_gain_and_r()
        sort_w_codes(0, LOGMAG)
        quantize_x(0)
        sort_w_codes(0, PHASE)
        magnitude(0, 0)
        project_next_phase()
        group_x(1, 0)
        group_x(1, 1)
        project_next_phase()
        magnitude(0, 1)
        project_next_phase()
        sort_w_codes(1, LOGMAG)
        sort_w_codes(1, PHASE)
        write(weave(phases(0)[:2], magnitudes(0)[2:]))
        quantize_x(1)
        write(weave(magnitudes(1, 2), phases(0)[2:] + phases(1)))
        write(cosines(0) + cosines(1))
        for u in range(2, G):
            sort_w_codes(u, LOGMAG)
            sort_w_codes(u, PHASE)
        early = magnitudes(3, 4, 5)
        write(early[:BANKS["side"]])
        sbuf_work(1)

        exps = {EARLY_EXP: early[BANKS["side"]:], LATE_EXP: magnitudes(6, 7)}
        to_turn = []
        for s in range(2, STEPS):
            groups = groups_of(s)
            share = share_of(s - 1)
            regroup = [(group_h_share, s - 1, share)] if share else []
            if share:
                multiply_h_share(s - 1, share)
            if len(groups) == 1:
                reads = phases(s)[:3] + weave(finishes(groups), phases(s)[3:])
            else:
                reads = weave(finishes(groups), phases(s))
            if s in exps:
                write(weave(reads, exps[s][:SLOTS] + regroup + exps[s][SLOTS:]))
                write(roundings(groups) + cosines(s))
            else:
                write(reads)
                write(regroup + weave(cosines(s), roundings(groups)))
            to_turn.extend(groups)
            if s != EARLY_EXP:
                write(turnings(to_turn))
                to_turn.clear()
            sbuf_work(s)

        synth_free.extend(["phase"] * BANKS["phase"])
        synthesize_next()
        quantize_y(LAST - 3, 0, FRAMES)
        store_scales(0, LAST - 2, [nc.sync] * QUADRANTS)
        multiply_h(LAST, 0, GROUP)
        multiply_h(LAST, GROUP, FRAMES)
        quantize_h(LAST, 0, GROUP)
        quantize_h(LAST, GROUP, FRAMES)
        on_gpsimd = groups_of(STEPS)
        on_vector = [(LAST - 1, 1), (LAST, 0), (LAST, 1)]
        write(finishes(on_gpsimd))
        sums = {(s, tile): add_residual(s, tile) for s, g in on_vector for tile in (2 * g, 2 * g + 1)}
        write(roundings(on_gpsimd) + turnings(on_gpsimd))
        for s, g in on_vector:
            for tile in (2 * g, 2 * g + 1):
                apply_gain(s, tile, sums[s, tile], nc.vector)
            for tile in (2 * g, 2 * g + 1):
                round_y(s, tile, nc.vector.tensor_copy if s == LAST else nc.scalar.copy)
            write(turnings([(s, g)]))
        quantize_y(LAST - 2, 0, FRAMES)
        quantize_y(LAST - 1, 0, FRAMES)
        quantize_y(LAST, 0, GROUP)
        quantize_y(LAST, GROUP, FRAMES)
        store_scales(LAST - 2, STEPS, [nc.scalar, nc.sync, nc.scalar, nc.sync])
